import numpy as np, ml_dtypes
CORES = [16,17,18,19,32,33,34,35]
N = 8
BF = ml_dtypes.bfloat16
def gentries(a):
    return np.ascontiguousarray(a.reshape(8, 16, -1).transpose(0, 2, 1)).reshape(8, -1)
def gtable(e):
    e = np.asarray(e); return np.ascontiguousarray(e.reshape(8, -1, 16).transpose(0, 2, 1)).reshape(128, -1).astype(np.int32)
V, R, M, RO, P, H, CAP, NEED = 4096, 2816, 2, 3, 4, 2, 128, 9
S, TOP = V // N, 2 ** 20 - 1
def parts(rng):
    base = rng.integers(0, 2 ** 20, (1, 8, 16, 1)); amp = np.exp2(10 + 7 * rng.random((N, 8, 1, R)))
    x = np.clip(base + amp * rng.standard_normal((N, 8, 16, R)), 0, TOP).astype(np.int64)
    t = (np.exp2(14 + 3.5 * rng.random((N, 8, 1, 1))) * (0.5 + rng.random((N, 8, 16, 1)))).astype(np.int64)
    lv = rng.integers(0, V, (N, 8, P, R)); lv = np.where(rng.random((N, 8, 1, R)) < 0.5, np.sort(lv, axis=2), lv)
    cd = rng.integers(0, R, (N, 8, RO, M, V))
    return x, t, lv, cd
def pack(x, t, lv, cd):
    return {"px": np.ascontiguousarray(x.reshape(N, 128, R)).astype(np.int32), "th": np.ascontiguousarray(t.reshape(N, 128, 1)).astype(np.int32),
            "ray": np.stack([gtable(a.reshape(8, -1)) for a in lv]), "cand": np.stack([gtable(a.reshape(8, -1)) for a in cd])}
def setup_inputs(rng):
    return pack(*parts(rng))
def setup_inputs_room(rng):
    x, t, lv, cd = parts(rng); h = R // 8
    t = rng.integers(2 ** 14, 2 ** 15, (N, 8, 16, 1)); x = rng.integers(2 ** 18, 2 ** 19, (1, 8, 16, 1)) + rng.integers(0, 2 ** 13, (N, 8, 16, R))
    inc = np.zeros((8, V), bool); own = np.arange(V) // S
    for o in range(N):
        for g in range(8):
            n = int(rng.choice(np.array([0, 1, CAP - 1, CAP, CAP + 1, S]))); last = o == N - 1 and g < 4
            if o == 0: n = (CAP, CAP + 1, S, CAP - 1, 1, 0, CAP, CAP + 1)[g]
            if last: n = (CAP, 1, CAP - 1, CAP)[g]
            s = rng.permutation(S)[:n]
            if last and not np.any(s == S - 1): s[0] = S - 1
            inc[g, o * S + s] = True
    for a in range(N):
        for g in range(8):
            o = rng.permutation(R); hot, watch, calm = o[:h], o[h:2 * h], o[h:]
            m = np.argsort(rng.random((16, h)), axis=0) < rng.integers(NEED, 17, h)
            x[a, g][:, hot] += m * (rng.choice(np.array([-1, 1]), h) * rng.integers(2 ** 16, 2 ** 17, h))
            lv[a, g, 0, o[:2 * h]] = V - 1; cd[a, g, 0] = rng.choice(calm, (M, V))
            for who, back in ((hot, 1), (watch, 2)):
                v = np.flatnonzero(inc[g] & ((own + back) % N == a))
                cd[a, g, 0, rng.integers(0, M, len(v)), v] = rng.choice(who, len(v))
    return pack(x, t, lv, cd)
def setup_inputs_ties(rng):
    x, t, lv, cd = parts(rng); n = min(R // 8, S)
    base = rng.choice(np.array([0, 2 ** 19, TOP]), 8); base[0] = 0; base[1] = TOP; base[2] = 2 ** 19; sg = np.where(base > 2 ** 19, -1, 1)
    t = rng.choice(np.array([0, 1, 1000, 2 ** 18, 2 ** 19 - 8]), (N, 8, 1, 1)) + rng.integers(0, 3, (N, 8, 16, 1))
    x = np.tile(base.reshape(1, 8, 1, 1), (N, 1, 16, R))
    for a in range(N):
        for g in range(8):
            o = rng.permutation(R); hot, watch, calm = o[:n], o[n:2 * n], o[n:]; b, e = (a - 1) % N, (a - 2) % N
            m = (np.argsort(rng.random((16, n)), axis=0) < rng.choice(np.array([NEED - 1, NEED, 16]), n)).astype(np.int64)
            x[a, g][:, hot] = base[g] + sg[g] * (t[b, g] + m)
            v = b * S + rng.permutation(S)[:n]
            lv[a, g, 0, hot] = np.where(rng.random(n) < 0.4, v, np.where(rng.random(n) < 0.5, V - 1, np.maximum(v - 1, 0)))
            lv[a, g, 0, watch] = V - 1
            cd[a, g, 0] = rng.choice(calm, (M, V)); cd[a, g, 0, 0, v] = hot
            cd[a, g, 0, M - 1, e * S:(e + 1) * S] = rng.choice(watch, S)
    return pack(x, t, lv, cd)
def setup_inputs_alike(rng):
    x, t, lv, cd = parts(rng)
    cd[:, ::4] = rng.choice(np.array([0, R - 1, R // 2, 5]), (N, 2, RO, M, V)); cd[:, 3] = cd[:, 3][:, :, :1]
    lv[:, 1::2] = lv[:, 1::2, :1]
    lv[:, 2] = rng.choice(np.array([0, V - 1]), (N, P, R)); lv[:, 6] = rng.integers(0, 16, (N, P, R))
    return pack(x, t, lv, cd)
def setup_inputs_dim(rng):
    x, t, lv, cd = parts(rng); q = rng.permutation(N); k = int(rng.integers(0, 7)); o = int(q[1])
    lv[:, k] = lv[:, k] // 2; lv[q[0], :7] = rng.integers(0, 4, (7, P, R)); t[o] = TOP; t[q[2]] = 0
    for a, pixel in ((int(q[0]), 0), (int(q[3]), TOP)):
        s = rng.permutation(R)[:R // 16]; x[a, 7][:, s] = pixel; lv[a, 7, 0, s] = V - 1
        cd[a, 7, 0, 0, o * S:(o + 1) * S] = rng.choice(s, S)
    return pack(x, t, lv, cd)
def setup_inputs_spread(rng):
    x, t, lv, cd = parts(rng)
    t = np.minimum(np.exp2(10 + 10 * rng.random((N, 8, 16, 1))).astype(np.int64), TOP)
    x = np.minimum((np.exp2(20 * rng.random((N, 8, 1, R))) * rng.random((N, 8, 16, R))).astype(np.int64), TOP)
    return pack(x, t, lv, cd)
def check_inputs(d):
    bad = []
    for k, lo, hi in (("px", 0, TOP), ("th", 0, TOP), ("ray", 0, V - 1), ("cand", 0, R - 1)):
        if np.min(d[k]) < lo or np.max(d[k]) > hi: bad.append("range of " + k)
    return bad
def reference(px, th, ray, cand):
    x = px.astype(np.int64).reshape(N, 8, 16, R); t = th.astype(np.int64).reshape(N, 8, 16, 1)
    lv = np.stack([gentries(a) for a in ray]).astype(np.int64).reshape(N, 8, P, R)
    cd = np.stack([gentries(a) for a in cand]).astype(np.int64).reshape(N, 8, RO, M, V)
    c = np.zeros((N, 8, R), np.int64); number = np.arange(V)
    for rnd in range(RO):
        w = np.take_along_axis(lv, c[:, :, None, :], 2)[:, :, 0]
        lo = np.full((8, 16, V), TOP + 1, np.int64); hi = np.full((8, 16, V), -1, np.int64)
        for a in range(N):
            for m in range(M):
                ix = cd[a, :, rnd, m]
                sees = (number <= np.take_along_axis(w[a], ix, 1))[:, None, :]
                v = np.take_along_axis(x[a], ix[:, None, :], 2)
                lo = np.minimum(lo, np.where(sees, v, TOP + 1)); hi = np.maximum(hi, np.where(sees, v, -1))
        carved = np.zeros((8, V), bool)
        for o in range(N):
            far = (hi[:, :, o * S:(o + 1) * S] - lo[:, :, o * S:(o + 1) * S] > t[o]).astype(np.int64)
            odd = np.add.reduce(far, axis=1) >= NEED
            carved[:, o * S:(o + 1) * S] = odd & (np.add.accumulate(odd.astype(np.int64), axis=1) <= CAP)
        for step in range(H):
            w = np.take_along_axis(lv, c[:, :, None, :], 2)[:, :, 0]
            nx, nc = [], []
            for a in range(N):
                gone = np.take_along_axis(carved, w[a], 1); e = np.take_along_axis(lo, w[a][:, None, :], 2)
                nx.append(np.where(gone[:, None, :], np.clip(x[a] + ((x[a] - e) >> 2), 0, TOP), x[a]))
                nc.append(np.minimum(c[a] + gone.astype(np.int64), P - 1))
            x = np.stack(nx); c = np.stack(nc)
    yc = np.stack([gtable(c[a]) for a in range(N)])
    return {"yx": x.reshape(N, 128, R).astype(np.float32), "yc": yc.astype(np.float32)}

@@ -1,0 +1,505 @@
+from concourse.bass import DstId, RemoteDMATransfer
+from concourse.mybir import dt, AluOpType, AxisListType, ActivationFunctionType
+
+A = AluOpType
+F = ActivationFunctionType
+R, V, TOP, BIG = 2816, 4096, 2 ** 20 - 1, 2 ** 22
+U = 4096.0
+NC = 4
+PIECES = ((0, 96), (96, 176))
+LOOK = "vsss"
+CUT = 96
+f32, i32, u16, f16, b16 = "float32", "int32", "uint16", "float16", "bfloat16"
+SCRATCH = {n: ("sbuf", [128] + list(sh), d) for n, sh, d in (
+    ("sta", (2, 8, 4, 8), i32), ("stb", (4, 8, 4, 8), i32), ("stc", (4, 8, 4, 8), i32), ("str0", (176,), i32),
+    ("str1", (528,), i32), ("sth", (1,), i32), ("sth2", (2,), i32), ("ls0", (696,), u16), ("ls1", (2048,), u16),
+    ("lsr", (528,), u16), ("ll0", (696,), u16), ("ll1", (2048,), u16), ("llr", (528,), u16),
+    ("ia", (128,), i32), ("ib", (128,), i32), ("ic", (128,), i32), ("io2", (256,), i32), ("io3", (256,), i32),
+    ("uk", (16, 128), f16), ("dkb", (16, 128), b16), ("dkf", (16, 128), f32), ("ob", (128,), b16), ("ni", (128,), b16),
+    ("pmx", (128,), f32), ("idf", (128,), f32), ("ones", (512,), b16), ("six", (128,), b16), ("vt", (4096,), f32),
+    ("vp", (256,), f32), ("nth", (1,), f32), ("thf", (4,), f32),
+    ("xi", (2816,), i32), ("xf", (2824,), f32), ("xl", (2824,), f32), ("w", (2816,), f32), ("wf", (176,), f32),
+    ("wu", (176,), u16), ("w16", (176,), f16), ("cur", (176,), f32), ("dl", (528,), f32), ("q1", (352,), f32),
+    ("q2", (176,), f32), ("eq", (528,), f32), ("pr", (528,), f32), ("cfin", (176,), f32),
+    ("cf", (512,), f32), ("wg0", (1024,), f32), ("wg1", (1024,), f32), ("mk0", (1024,), b16), ("mk1", (1024,), b16),
+    ("sm", (256,), f32), ("oo", (512,), u16), ("zb0", (1024,), f32), ("zb1", (1024,), f32), ("hb0", (1024,), f32),
+    ("hb1", (1024,), f32), ("lb0", (1024,), f32), ("lb1", (1024,), f32), ("zz", (8, 4, 2, 128), f32), ("hs", (512,), f32),
+    ("fe", (512,), f32), ("far", (512,), b16), ("inc", (512,), b16), ("cum", (512,), f32), ("pc", (512,), b16),
+    ("et", (512,), f32), ("ea", (4096,), f32), ("ag", (2816,), f32), ("sg", (2816,), b16), ("tq", (176,), f32))}
+SCRATCH.update({n: ("dram", list(sh), d) for n, sh, d in (
+    ("l0d", (8, 128, 87), u16), ("l0r", (8, 128, 87), u16), ("l1d", (8, 128, 256), u16), ("l1r", (8, 128, 256), u16),
+    ("lrd", (8, 128, 66), u16), ("lrr", (8, 128, 66), u16), ("pxd", (16, 128, 176), i32), ("pxr", (16, 128, 176), i32),
+    ("rb", (4, 128, 176), i32), ("ro", (4, 128, 192), f32), ("od0", (8, 128, 192), f32), ("or0", (8, 128, 192), f32),
+    ("od1", (8, 128, 160), f32), ("or1", (8, 128, 160), f32), ("cd", (8, 128, 22), f32), ("cr", (8, 128, 22), f32))})
+SCRATCH.update({n: ("psum", [128, k], f32) for n, k in (("pb", 3072), ("pw", 512), ("pv", 512))})
+PSUM = ["pb%d" % k for k in range(6)] + ["pw", "pv"]
+SEMAPHORES = (["v", "s", "t", "gc", "lsem", "l0a", "l1a", "lra", "ca", "rbi", "roi", "rlo"]
+              + [n + str(q) for n in ("pxa", "oa", "ob") for q in range(8)] + [n + str(c) for n in ("rg", "rk") for c in range(NC)]
+              + ["ea0", "ea1", "dst", "dst1", "dl0", "dl1", "dpx", "dpy", "dlb", "dlc", "dxi", "dod0", "dod1", "dcd", "dy", "dz",
+                 "dsx", "dlr", "dlq"])
+
+
+def layout(T, topo):
+    lay = []
+    for r, c in enumerate(T.cores):
+        mine = [q for q, d in enumerate(T.cores) if topo.chip(d) == topo.chip(c)]
+        far = [q for q in range(len(T.cores)) if q not in mine]
+        other = [d for d in topo.cores_of(c) if topo.die(d) != topo.die(c)]
+        lay.append(([q for q in mine if q != r], far, other[mine.index(r)]))
+    return lay
+
+
+def two(engines, n):
+    return [(1 << engines[2 * k]) | (1 << engines[2 * k + 1]) for k in range(n)]
+
+
+def transfer(topo, dst, mask, src, out, sem):
+    rid, pid, _ = topo.addr(dst)
+    return RemoteDMATransfer(dst_ids=[DstId(rid=rid, pnc=pid)], dma_engine_mask=mask, remote_sem=sem, src=src, dst=out)
+
+
+def relay_program(g, core, T, topo, r, far):
+    masks = two(topo.engines(core, T.cores[far[0]]), len(far))
+    n = 2 * len(far)
+    for s, src, dst, to in (("rbi", T.rb, T.pxr[2 * r + 1], "pxa"), ("roi", T.ro, T.or0[r], "oa")):
+        g.wait_ge(T.sem[s], n)
+        g.remote_dma_fused([transfer(topo, T.cores[q], masks[k], src[k], dst, T.sem[to + str(r)]) for k, q in enumerate(far)],
+                           local_sem=T.sem.rlo)
+    g.wait_ge(T.sem.rlo, 2 * n)
+
+
+def rank_program(g, core, T, topo):
+    lay = layout(T, topo)
+    rank = T.rank_of(core)
+    if rank is None:
+        for r, (near, far, rel) in enumerate(lay):
+            if rel == core:
+                relay_program(g, core, T, topo, r, far)
+        return
+    near, far, rel = lay[rank]
+    sem = T.sem
+    queue = {"v": g.vector, "s": g.scalar, "t": g.tensor, "y": g.sync, "g": g}
+    own = {"v": "v", "s": "s", "t": "t", "g": "gc"}
+    cnt, seen, wr, rd = {}, {}, {}, {}
+
+    def waits(q, deps):
+        need = {}
+        for s, n in deps:
+            need[s] = max(need.get(s, 0), n)
+        for s in need:
+            if seen.get((q, s), 0) < need[s]:
+                queue[q].wait_ge(sem[s], need[s])
+                seen[(q, s)] = need[s]
+
+    def deps_of(q, reads, writes):
+        d = []
+        for k in reads + writes:
+            d += wr.get(k, [])
+        for k in writes:
+            d += rd.get(k, {}).items()
+        for k in reads:
+            if k in PSUM:
+                d += [(s, n) for s, n in rd.get(k, {}).items() if s != own.get(q)]
+        return d
+
+    def done(tag, reads, writes):
+        for k in reads:
+            rd.setdefault(k, {})[tag[0]] = tag[1]
+        for k in writes:
+            wr[k] = [tag]
+            rd[k] = {}
+
+    calls = {"act": g.scalar.activation, "iota": g.iota, "copy": g.vector.tensor_copy, "tt": g.vector.tensor_tensor,
+             "ts": g.vector.tensor_scalar, "set": g.vector.memset, "scan": g.vector.tensor_tensor_scan}
+
+    def op(q, name, args, reads, writes, **kw):
+        waits(q, deps_of(q, reads, writes))
+        s = own[q]
+        if name == "mm":
+            for a in args:
+                ins = g.tensor.matmul(*a)
+        else:
+            ins = calls[name](*args, **kw)
+        cnt[s] = cnt.get(s, 0) + 1
+        ins.then_inc(sem[s], 1)
+        done((s, cnt[s]), reads, writes)
+
+    def vts(out, in0, s1, s2, ops, reads, writes):
+        op("v", "ts", (out, in0, s1, s2) + ops, reads, writes)
+
+    def dma(q, pairs, s, reads, writes):
+        waits(q, deps_of(q, reads, writes))
+        for o, i in pairs:
+            queue[q].dma_start(o, i).then_inc(sem[s], 16)
+        cnt[s] = cnt.get(s, 0) + 16 * len(pairs)
+        done((s, cnt[s]), reads, writes)
+
+    def arrives(s, n, key):
+        cnt[s] = cnt.get(s, 0) + n
+        wr[key] = [(s, cnt[s])]
+
+    nf, nn = len(far), len(near)
+    off = topo.engines(core, T.cores[far[0]])
+    rest = [e for e in topo.engines(core, T.cores[near[0]]) if e not in off]
+
+    def send(moves, reads):
+        waits("g", deps_of("g", reads, []))
+        g.remote_dma_fused([transfer(topo, d, m, a, b, sem[s]) for d, m, a, b, s in moves], local_sem=sem.lsem)
+        cnt["lsem"] = cnt.get("lsem", 0) + 2 * len(moves)
+
+    def to_far(src, dst, s):
+        return [(T.cores[q], m, src(q), dst, s) for q, m in zip(far, two(off, nf))]
+
+    def to_relay(src, via, vsem):
+        return [(rel, m, src(q), via[k], vsem) for k, (q, m) in enumerate(zip(far, two(rest, nf)))]
+
+    def to_near(src, dst, s, engines):
+        return [(T.cores[q], m, src(q), dst, s) for q, m in zip(near, two(engines, nn))]
+
+    def to_all(src, dst, s):
+        return to_far(lambda q: src[q], dst[rank], s) + to_near(lambda q: src[q], dst[rank], s, rest)
+
+    lo, hi = 16 * rank, 16 * rank + 16
+    npc = range(len(PIECES))
+    others = [(a, b) for a, b in ((0, rank), (rank + 1, 8)) if b > a]
+
+    def land(q, dst, src, mine, s, reads, key):
+        dma(q, [(dst[16 * a:16 * b, :], src[a:b]) for a, b in others] + [(dst[lo:hi, :], mine[lo:hi, :])], s, reads, [key])
+
+    dma("y", [(T.sta[:], T.cand[:, 0:512]), (T.str0[:], T.ray[:, 0:176]), (T.sth[:], T.th[:])], "dst", [], ["sta", "str0", "sth"])
+    fa, fb = far[0], far[-1] + 1
+    na, nb = min(near + [rank]), max(near + [rank]) + 1
+    dma("y", [(T.pxd[2 * fa:2 * fb], T.px[16 * fa:16 * fb, :])], "dpx", [], ["pxdf"])
+    op("g", "iota", (T.ia[:], [[-16, 8], [0, 16]], 0, 1), [], ["ia"])
+    op("g", "iota", (T.ib[:], [[-16000, 8], [-999, 16]], 0, 1000), [], ["ib"])
+    op("g", "iota", (T.vt[:, 0:1024], [[512, 8], [1, 128]], -2048, 0), [], ["vt0"], allow_small_or_imprecise_dtypes=True)
+
+    def selectors(ks):
+        for k in ks:
+            vts(T.uk[:, k, :], T.ia[:], float(k), None, (A.is_equal,), ["ia"], ["uk" if k == 15 else "uk.%d" % k])
+
+    op("v", "set", (T.ls0[:, 688:696], 0), [], ["ls0"])
+    selectors(range(8))
+    for m in range(2):
+        for c in range(NC):
+            k = c * 128 + m * 64
+            op("v", "copy", (T.ls0[:, k:k + 64], T.sta[:, m, :, c, :]), ["sta"], ["ls0.%d" % k])
+    op("v", "copy", (T.ls0[:, 512:688], T.str0[:]), ["str0"], ["ls0.r"])
+    vts(T.sth2[:, 0:1], T.sth[:], 10, None, (A.arith_shift_right,), ["sth"], ["sth2a"])
+    vts(T.sth2[:, 1:2], T.sth[:], 1023, None, (A.bitwise_and,), ["sth"], ["sth2b"])
+    op("v", "copy", (T.ls0[:, 688:690], T.sth2[:]), ["sth2a", "sth2b"], ["ls0"])
+    ls0k = ["ls0", "ls0.r"] + ["ls0.%d" % k for k in range(0, 512, 64)]
+    dma("y", [(T.l0d[:], T.ls0[:])], "dlb", ls0k, ["l0d"])
+    dma("y", [(T.pxd[2 * na:2 * nb], T.px[16 * na:16 * nb, :])], "dpy", [], ["pxdn"])
+    dma("y", [(T.str1[:], T.ray[:, 176:704]), (T.stb[:], T.cand[:, 512:1536])], "dst1", [], ["stb", "str1"])
+    send(to_all(T.l0d, T.l0r, "l0a"), ["l0d"])
+    ps = "pxa%d" % rank
+    send(to_relay(lambda q: T.pxd[2 * q + 1], T.rb, "rbi") + to_far(lambda q: T.pxd[2 * q], T.pxr[2 * rank], ps), ["pxdf"])
+    send(to_near(lambda q: T.pxd[2 * q], T.pxr[2 * rank], ps, rest)
+         + to_near(lambda q: T.pxd[2 * q + 1], T.pxr[2 * rank + 1], ps, off), ["pxdn"])
+    selectors(range(8, 16))
+    for k in range(16):
+        vts(T.dkf[:, k, :], T.ib[:], float(k), -U, (A.is_equal, A.mult), ["ib"], ["dkf" if k == 15 else "dkf.%d" % k])
+    op("v", "copy", (T.dkb[:], T.dkf[:]), ["dkf"], ["dkb"])
+    for c in range(1, NC):
+        vts(T.vt[:, 1024 * c:1024 * c + 1024], T.vt[:, 0:1024], 128.0 * c, None, (A.add,), ["vt0"], ["vt%d" % c])
+    op("g", "iota", (T.io2[:], [[128, 4], [512, 8], [16, 8]], -2048, 0), [], ["io2"])
+    op("g", "iota", (T.io3[:], [[0, 256]], 0, 1), [], ["io3"])
+    op("g", "iota", (T.ia[:], [[-1, 16], [-16, 8]], 0, 1), [], ["ia"])
+    op("g", "iota", (T.ib[:], [[-1, 128]], 0, 1), [], ["ib"])
+    op("g", "iota", (T.ic[:], [[0, 16], [1, 8]], 1024, -1), [], ["ic"])
+    vts(T.io3[:], T.io3[:], 15, None, (A.bitwise_and,), ["io3"], ["io3"])
+    vts(T.ic[:], T.ic[:], 7, None, (A.bitwise_and,), ["ic"], ["ic"])
+    op("v", "tt", (T.io2[:], T.io2[:], T.io3[:], A.add), ["io2", "io3"], ["io2"])
+    vts(T.pmx[:], T.ia[:], 0.0, None, (A.is_equal,), ["ia"], ["pmx"])
+    vts(T.idf[:], T.ib[:], 0.0, None, (A.is_equal,), ["ib"], ["idf"])
+    vts(T.ni[:], T.ib[:], 0.0, -0.25, (A.is_equal, A.mult), ["ib"], ["ni"])
+    vts(T.ob[:], T.ic[:], 0.0, None, (A.is_equal,), ["ic"], ["ob"])
+    vts(T.vp[:], T.io2[:], U, None, (A.mult,), ["io2"], ["vp"])
+    op("v", "set", (T.ones[:], 1.0), [], ["ones"])
+    op("v", "set", (T.six[:], 64.0), [], ["six"])
+    op("v", "set", (T.xl[:, 2816:2824], float(BIG)), [], ["xls"])
+    op("v", "set", (T.xf[:, 2816:2824], float(-BIG)), [], ["xfs"])
+    op("v", "set", (T.cur[:], 0.0), [], ["cur%d" % p for p in npc])
+    op("v", "copy", (T.lsr[:], T.str1[:]), ["str1"], ["lsr"])
+    dma("s", [(T.lrd[:], T.lsr[:])], "dlr", ["lsr"], ["lrd"])
+    arrives("l0a", 14, "l0r")
+    land("y", T.ll0, T.l0r, T.ls0, "dl0", ["l0r"] + ls0k, "ll0")
+    send(to_all(T.lrd, T.lrr, "lra"), ["lrd"])
+    w16k, wfk, curk = ["w16.%d" % p for p in npc], ["wf%d" % p for p in npc], ["cur%d" % p for p in npc]
+    vts(T.w16[:], T.ll0[:, 512:688], -2048.0, None, (A.add,), ["ll0"], w16k)
+    op("v", "copy", (T.wf[:], T.ll0[:, 512:688]), ["ll0"], wfk)
+
+    def later_lists():
+        vts(T.stc[:], T.stb[:], 4, None, (A.arith_shift_right,), ["stb"], ["stc"])
+        for half in range(2):
+            for m in range(4):
+                for c in range(NC):
+                    k = half * 1024 + (m // 2) * 512 + c * 128 + (m % 2) * 64
+                    op("v", "copy", (T.ls1[:, k:k + 64], T.stb[:, m, :, c, :]), ["stb"], ["ls1.%d" % k])
+            if half == 0:
+                vts(T.stb[:], T.stb[:], 15, None, (A.bitwise_and,), ["stb"], ["stb"])
+                vts(T.stb[:], T.stb[:], 176.0, None, (A.mult,), ["stb"], ["stb"])
+                op("v", "tt", (T.stb[:], T.stb[:], T.stc[:], A.add), ["stb", "stc"], ["stb"])
+        ls1k = ["ls1.%d" % k for k in range(0, 2048, 64)]
+        dma("y", [(T.l1d[:], T.ls1[:])], "dlc", ls1k, ["l1d"])
+        send(to_all(T.l1d, T.l1r, "l1a"), ["l1d"])
+        arrives("l1a", 14, "l1r")
+        land("y", T.ll1, T.l1r, T.ls1, "dl1", ["l1r"] + ls1k, "ll1")
+
+    def thresholds():
+        op("v", "copy", (T.thf[:, 0:2], T.ll0[:, 688:690]), ["ll0"], ["thf"])
+        vts(T.thf[:, 2:3], T.thf[:, 0:1], 1024.0, None, (A.mult,), ["thf"], ["thf2"])
+        op("v", "tt", (T.thf[:, 3:4], T.thf[:, 2:3], T.thf[:, 1:2], A.add), ["thf", "thf2"], ["thf3"])
+        op("t", "mm", [(T.pb[:, 2048:2049], T.pmx[:], T.thf[:, 3:4], True, True)], ["pmx", "thf3"], ["pb4"])
+        vts(T.nth[:], T.pb[:, 2048:2049], -1.0, None, (A.mult,), ["pb4"], ["nth"])
+
+    dma("y", [(T.xi[lo:hi, :], T.px[lo:hi, :])], "dsx", [], ["xi.own"])
+    for q in near + far:
+        arrives("pxa%d" % q, 4, "pxr%d" % q)
+        dma("y", [(T.xi[16 * q:16 * q + 16, :], T.pxr[2 * q:2 * q + 2])], "dxi", ["pxr%d" % q], ["xi.%d" % q])
+    xik = ["xi.own", "xi.%d" % far[-1]]
+    wk = ["w%d" % b for b in range(8)]
+
+    def unpack(t):
+        if t == 0:
+            parts = [(512 * b, min(512 * b + 512, R)) for b in range(6)]
+        else:
+            parts = [(352 * b, 352 * b + 352) for b in range(8)]
+        for n, (a, b) in enumerate(parts):
+            ps, key = ((T.pw, "pw"), (T.pv, "pv"))[n % 2]
+            if t == 0:
+                mm = [(ps[:, k:b - a:16], T.uk[:, k, :], T.w16[:, a // 16:b // 16], True, True) for k in range(16)]
+            else:
+                mm = [(ps[:, 176 * k:176 * k + 176], T.uk[:, 2 * n + k, :], T.w16[:], True, True) for k in range(2)]
+            op("t", "mm", mm, ["uk"] + w16k, [key])
+            op("s", "act", (T.w[:, a:b], ps[:, 0:b - a], F.Copy), [key], [wk[n]])
+
+    def lists(t, where=0):
+        return (T.ll0, 0, "ll0") if t == 0 else (T.ll1, 512 * (t - 1) + 1024 * where, "ll1")
+
+    def prepare(t):
+        buf, base, key = lists(t)
+        op("v", "copy", (T.cf[:], buf[:, base:base + 512]), [key], ["cf"])
+
+    turn = [0]
+
+    def look(t, c, m, q):
+        buf, base, key = lists(t, 1)
+        k = base + c * 128 + m * 64
+        out, ok = T.pb[:, 512 * c + 64 * m:512 * c + 64 * m + 64], "pb%d" % c
+        win = T.w[:, 0:R].indirect(buf[:, k:k + 64])
+        if q == "s":
+            wg, wgk = (T.wg0, T.wg1)[c % 2], "wg%d" % (c % 2)
+            op("s", "act", (wg[:], win, F.Copy), [key] + wk, [wgk])
+            op("t", "mm", [(out, T.idf[:], T.vp[:, c * 64:c * 64 + 64], True, False)]
+               + [(out, T.dkf[:, i, :], wg[:, i:1024:16], False, i == 15) for i in range(16)], ["dkf", "idf", "vp", wgk], [ok])
+        else:
+            turn[0] ^= 1
+            mk, mkk = (T.mk0, T.mk1)[turn[0]], "mk%d" % turn[0]
+            op("v", "tt", (mk[:], win, T.vt[:, c * 1024:c * 1024 + 1024], A.is_ge), [key, "vt%d" % c] + wk, [mkk])
+            op("t", "mm", [(out, T.six[0:1, :], T.six[0:1, 0:64], True, False)]
+               + [(out, T.dkb[:, i, :], mk[:, i:1024:16], False, i == 15) for i in range(16)], ["dkb", "six", mkk], [ok])
+
+    def mask(c):
+        d, e, k = slice(c * 128, c * 128 + 128), slice(c % 2 * 128, c % 2 * 128 + 128), "sm%d" % (c % 2)
+        op("v", "tt", (T.sm[:, e], T.pb[:, 512 * c:512 * c + 128], T.cf[:, d], A.max), ["pb%d" % c, "cf"], [k])
+        vts(T.oo[:, d], T.sm[:, e], float(R), None, (A.min,), [k], ["oo%d" % c])
+
+    xfk = ["xf%d" % p for p in npc] + ["xfs"]
+    xlk = ["xl%d" % p for p in npc] + ["xls"]
+
+    def see0(c):
+        e, d = c % 2, slice(c * 128, c * 128 + 64)
+        for z, f, n in ((T.ag[:, 1024 * e:1024 * e + 1024], F.Copy, ["za%d" % e] + ["ag%d" % p for p in npc]),
+                        ((T.zb0, T.zb1)[e][:], F.Abs, ["zb%d" % e])):
+            op("s", "act", (z, T.xf[:, 0:2824].indirect(T.oo[:, d]), f), ["oo%d" % c] + xfk, n)
+
+    def see1(c):
+        e, d = c % 2, slice(c * 128 + 64, c * 128 + 128)
+        za, zb, hb, lb = T.ag[:, 1024 * e:1024 * e + 1024], (T.zb0, T.zb1)[e], (T.hb0, T.hb1)[e], (T.lb0, T.lb1)[e]
+        op("v", "tt", (hb[:], T.xf[:, 0:2824].indirect(T.oo[:, d]), za, A.max), ["oo%d" % c, "za%d" % e] + xfk, ["hb%d" % e])
+        dma("y", [(T.zz[:, a, c, 0, :], hb[16 * a:16 * a + 16, :]) for a in range(8)], "rg%d" % c, ["hb%d" % e], ["zh%d" % c])
+        op("v", "tt", (lb[:], T.xl[:, 0:2824].indirect(T.oo[:, d]), zb[:], A.min), ["oo%d" % c, "zb%d" % e] + xlk, ["lb%d" % e])
+        dma("y", [(T.zz[:, a, c, 1, :], lb[16 * a:16 * a + 16, :]) for a in range(8)], "rk%d" % c, ["lb%d" % e], ["zl%d" % c])
+
+    def reduce(c0, c1):
+        for a in range(1, 8):
+            for j, o, z in ((0, A.max, "zh"), (1, A.min, "zl")):
+                b = 2048 + 512 * j
+                acc, key = T.pb[:, b + 128 * c0:b + 128 * c1], "pb%d" % (4 + j)
+                x, src = T.zz[:, a, c0:c1, j, :], [z + str(c) for c in range(c0, c1)]
+                if a == 1:
+                    op("v", "tt", (acc, T.zz[:, 0, c0:c1, j, :], x, o), src, [key])
+                else:
+                    op("v", "tt", (acc, acc, x, o), src + [key], [key])
+
+    def carve():
+        op("s", "act", (T.hs[:], T.pb[:, 2048:2560], F.Identity, T.nth[:]), ["pb4", "nth"], ["hs"])
+        op("v", "tt", (T.far[:], T.hs[:], T.pb[:, 2560:3072], A.is_gt), ["hs", "pb5"], ["far"])
+        op("s", "act", (T.fe[:], T.pb[:, 2560:3072], F.Copy, -0.375, -0.25), ["pb5"], ["fe"])
+        op("t", "mm", [(T.pw[:], T.ob[:], T.far[:], True, True)], ["ob", "far"], ["pw"])
+        vts(T.inc[:], T.pw[:], 9.0, None, (A.is_ge,), ["pw"], ["inc"])
+        op("v", "scan", (T.cum[:], T.inc[:], T.inc[:], 0.0, A.add, A.max), ["inc"], ["cum"])
+        op("v", "tt", (T.pv[:], T.inc[:], T.fe[:], A.mult), ["inc", "fe"], ["pv"])
+        vts(T.pc[:], T.cum[:], 128.0, None, (A.is_le,), ["cum"], ["pc"])
+        op("v", "tt", (T.et[:], T.pc[:], T.pv[:], A.mult), ["pc", "pv"], ["et"])
+        dma("y", [(T.ea[16 * a:16 * a + 16, :], T.et[:]) for a in range(0, 4)], "ea0", ["et"], ["eaa"])
+        dma("s", [(T.ea[16 * a:16 * a + 16, :], T.et[:]) for a in range(4, 8)], "ea1", ["et"], ["eab"])
+
+    dl = T.dl
+
+    def places(t):
+        if t == 0:
+            op("v", "copy", (T.eq[:], T.llr[:]), ["llr"], ["eq0", "eq1", "eq2"])
+            op("v", "tt", (T.pr[:, 0:176], T.eq[:, 0:176], T.wf[:], A.subtract), ["eq0"] + wfk, ["pr.0"])
+            op("v", "tt", (T.pr[:, 176:528], T.eq[:, 176:528], T.eq[:, 0:352], A.subtract), ["eq0"], ["pr"])
+            vts(dl[:], T.pr[:], 1.0 / U, None, (A.mult,), ["pr.0", "pr"], ["dl"])
+            return
+        for k in range(3):
+            vts(T.eq[:, k * 176:k * 176 + 176], T.cur[:], U * k, None, (A.is_equal,), curk, ["eq%d" % k])
+        op("v", "tt", (T.pr[:], T.eq[:], dl[:], A.mult), ["eq0", "eq1", "eq2", "dl"], ["pr"])
+        op("v", "tt", (T.q1[:, 176:352], T.pr[:, 0:176], T.pr[:, 176:352], A.add), ["pr"], ["q1t"])
+        op("v", "tt", (T.q1[:, 0:176], T.q1[:, 176:352], T.pr[:, 352:528], A.add), ["pr", "q1t"], ["q1"])
+        op("v", "tt", (T.pr[:, 0:352], T.eq[:, 0:352], dl[:, 176:528], A.mult), ["eq0", "eq1", "dl"], ["pr"])
+        op("v", "tt", (T.q2[:], T.pr[:, 0:176], T.pr[:, 176:352], A.add), ["pr"], ["q2"])
+
+    pgs = [((T.pw, "pw"), (T.pv, "pv"))[p % 2] for p in npc]
+
+    def span(p):
+        return 16 * PIECES[p][0], 16 * PIECES[p][1]
+
+    def banks(p):
+        a, b = span(p)
+        return [(k, 512 * k, min(512 * k + 512, R)) for k in range(a // 512, (b + 511) // 512)]
+
+    def gather(p, q):
+        a, b = span(p)
+        out, src = T.ag[:, a:b], T.ea[:, 0:V].indirect(T.wu[:, a // 16:b // 16])
+        args, name = ((out, src, F.Copy), "act") if q == "s" else ((out, src), "copy")
+        op(q, name, args, ["eaa", "eab", "wu%d" % p], ["ag%d" % p, "za0", "za1"])
+        op("s", "act", (T.sg[:, a:b], out, F.Sign), ["ag%d" % p], ["sg%d" % p])
+
+    def pack(p):
+        a, b = PIECES[p]
+        ps, key = pgs[p]
+        op("t", "mm", [(ps[:, a:b], T.dkb[:, k, :], T.sg[:, 16 * a + k:16 * b:16], k == 0, k == 15) for k in range(16)],
+           ["dkb", "sg%d" % p], [key])
+
+    def spread(p):
+        for k, x, y in banks(p):
+            op("t", "mm", [(T.pb[:, x:y], T.ones[0:1, 0:128], T.ones[0:1, 0:y - x], True, False),
+                           (T.pb[:, x:y], T.ni[:], T.sg[:, x:y], False, True)], ["ni", "ones", "sg%d" % p], ["pb%d" % k])
+
+    def small(p, t, step, last):
+        a, b = PIECES[p]
+        ps, key = pgs[p]
+        if t == 0:
+            q, qk = dl[:, 176 * step + a:176 * step + b], "dl"
+        else:
+            q, qk = (T.q1[:, a:b], "q1") if step == 0 else (T.q2[:, a:b], "q2")
+        wfp, tqp = ["wf%d" % p], ["tq%d" % p]
+        if not last:
+            op("v", "tt", (T.tq[:, a:b], ps[:, a:b], q, A.mult), [key, qk], tqp)
+            op("v", "tt", (T.wf[:, a:b], T.wf[:, a:b], T.tq[:, a:b], A.add), wfp + tqp, wfp)
+            if step == 1:
+                vts(T.w16[:, a:b], T.wf[:, a:b], -2048.0, None, (A.add,), wfp, ["w16.%d" % p])
+            op("v", "copy", (T.wu[:, a:b], T.wf[:, a:b]), wfp, ["wu%d" % p])
+        op("v", "tt", (T.cur[:, a:b], ps[:, a:b], T.cur[:, a:b], A.add), [key, "cur%d" % p], ["cur%d" % p])
+
+    def move(p, part):
+        a, b = span(p)
+        pk = ["pb%d" % k for k, _, _ in banks(p)]
+        if part == 0:
+            op("v", "tt", (T.pb[:, a:b], T.xf[:, a:b], T.pb[:, a:b], A.mult), pk + ["xf%d" % p], pk)
+        elif part == 1:
+            op("v", "tt", (T.xi[:, a:b], T.pb[:, a:b], T.ag[:, a:b], A.add), pk + ["ag%d" % p], ["xi%d" % p])
+        else:
+            vts(T.xf[:, a:b], T.xi[:, a:b], 0.0, float(TOP), (A.max, A.min), ["xi%d" % p], ["xf%d" % p])
+
+    def second(p):
+        a, b = span(p)
+        op("s", "act", (T.xl[:, a:b], T.xf[:, a:b], F.Copy), ["xf%d" % p], ["xl%d" % p])
+
+    op("v", "copy", (T.wu[:], T.wf[:]), wfk, ["wu%d" % p for p in npc])
+    unpack(0)
+    for t in range(3):
+        if t == 0:
+            prepare(0)
+            for c in range(NC):
+                look(0, c, 0, "v")
+                look(0, c, 1, "v")
+                if c:
+                    mask(c - 1)
+            mask(NC - 1)
+            thresholds()
+            for p in npc:
+                a, b = span(p)
+                op("v", "copy", (T.xf[:, a:b], T.xi[:, a:b]), xik, ["xf%d" % p])
+                second(p)
+            for c in range(NC):
+                see0(c)
+                see1(c)
+            arrives("lra", 14, "lrr")
+            land("y", T.llr, T.lrr, T.lsr, "dlq", ["lrr", "lsr"], "llr")
+        else:
+            for c in range(NC + 2):
+                if c < NC:
+                    look(t, c, 0, LOOK[c])
+                    look(t, c, 1, "v")
+                if 1 <= c <= NC:
+                    mask(c - 1)
+                    see0(c - 1)
+                if c >= 2:
+                    see1(c - 2)
+        reduce(0, NC - 1)
+        reduce(NC - 1, NC)
+        carve()
+        places(t)
+        if t == 0:
+            later_lists()
+        elif t == 1:
+            prepare(2)
+        for step in range(2):
+            end = step == 1
+            last = end and t == 2
+            gather(0, "s")
+            for p in npc[1:]:
+                gather(p, "s" if step or p > 1 else "v")
+            for p in npc:
+                pack(p)
+                spread(p)
+            small(0, t, step, last)
+            for p in npc:
+                move(p, 0)
+                if p + 1 < len(PIECES):
+                    small(p + 1, t, step, last)
+                elif last:
+                    vts(T.cfin[:], T.cur[:], 1.0 / U, 3.0, (A.mult, A.min), curk, ["cfin"])
+                move(p, 1)
+                move(p, 2)
+            if end and t < 2:
+                for p in npc[:-1]:
+                    second(p)
+                unpack(t + 1)
+                if t == 0:
+                    prepare(1)
+                second(npc[-1])
+    w0 = 16 * CUT
+    first = ["xf%d" % p for p in npc if PIECES[p][1] <= CUT]
+    later = ["xf%d" % p for p in npc if PIECES[p][1] > CUT]
+    dma("y", [(T.od0[:], T.xf[:, 0:w0])], "dod0", first, ["od0"])
+    dma("s", [(T.cd[:], T.cfin[:])], "dcd", ["cfin"], ["cd"])
+    dma("y", [(T.od1[:], T.xf[:, w0:R])], "dod1", later, ["od1"])
+    send(to_relay(lambda q: T.od0[q], T.ro, "roi") + to_near(lambda q: T.od0[q], T.or0[rank], "oa%d" % rank, off), ["od0"])
+    send(to_all(T.cd, T.cr, "ca"), ["cd"])
+    send(to_all(T.od1, T.or1, "ob%d" % rank), ["od1"])
+    dma("s", [(T.yx[lo:hi, 0:w0], T.xf[lo:hi, 0:w0]), (T.yx[lo:hi, w0:R], T.xf[lo:hi, w0:R]),
+              (T.yc[lo:hi, :], T.cfin[lo:hi, :])], "dz", first + later + ["cfin"], [])
+    arrives("ca", 14, "cr")
+    dma("s", [(T.yc[16 * a:16 * b, :], T.cr[a:b]) for a, b in others], "dz", ["cr"], [])
+    for s, src, dst, q0, d in (("oa", T.or0, slice(0, w0), "y", "dy"), ("ob", T.or1, slice(w0, R), "s", "dz")):
+        for q in near + far:
+            arrives(s + str(q), 2, s + ".%d" % q)
+            dma(q0, [(T.yx[16 * q:16 * q + 16, dst], src[q])], d, [s + ".%d" % q], [])
+    waits("g", [(s, cnt[s]) for s in cnt])

@@ -7,36 +7,38 @@ R, V, TOP, BIG = 2816, 4096, 2 ** 20 - 1, 2 ** 22
 U = 4096.0
 NC = 4
 PIECES = ((0, 96), (96, 176))
-LOOK = "vsss"
-CUT = 96
+KB = 3
+SCHED = "L00s L01v X0 L10s X1 L11v M0 Z0 M1 L20s V0 L21v Z1 L30s L31v M2 V1 Z2 M3 V2 Z3 V3 R03 R34"
 f32, i32, u16, f16, b16 = "float32", "int32", "uint16", "float16", "bfloat16"
 SCRATCH = {n: ("sbuf", [128] + list(sh), d) for n, sh, d in (
-    ("sta", (2, 8, 4, 8), i32), ("stb", (4, 8, 4, 8), i32), ("stc", (4, 8, 4, 8), i32), ("str0", (176,), i32),
-    ("str1", (528,), i32), ("sth", (1,), i32), ("sth2", (2,), i32), ("ls0", (696,), u16), ("ls1", (2048,), u16),
-    ("lsr", (528,), u16), ("ll0", (696,), u16), ("ll1", (2048,), u16), ("llr", (528,), u16),
-    ("ia", (128,), i32), ("ib", (128,), i32), ("ic", (128,), i32), ("io2", (256,), i32), ("io3", (256,), i32),
-    ("uk", (16, 128), f16), ("dkb", (16, 128), b16), ("dkf", (16, 128), f32), ("ob", (128,), b16), ("ni", (128,), b16),
-    ("pmx", (128,), f32), ("idf", (128,), f32), ("ones", (512,), b16), ("six", (128,), b16), ("vt", (4096,), f32),
-    ("vp", (256,), f32), ("nth", (1,), f32), ("thf", (4,), f32),
+    ("sta", (2, 8, 4, 8), i32), ("stb", (4, 8, 4, 8), i32), ("stc", (4, 8, 4, 8), i32), ("str", (704,), i32),
+    ("sth", (1,), i32), ("sth2", (2,), i32), ("ls0", (512,), u16), ("ls1", (2048,), u16),
+    ("lsr", (712,), u16), ("ll1", (2048,), u16), ("llr", (712,), u16), ("om", (512,), u16),
+    ("ia", (128,), i32), ("ib", (128,), i32), ("ic", (128,), i32), ("id", (128,), i32), ("ie", (128,), i32),
+    ("ig", (128,), i32), ("es", (3, 128), f32), ("io2", (64,), i32), ("io3", (64,), i32),
+    ("uk", (16, 128), f16), ("dkb", (16, 128), b16), ("ob", (128,), b16), ("ni", (128,), b16),
+    ("pmx", (128,), f32), ("ones", (512,), b16), ("six", (128,), b16), ("vt", (4096,), f32),
+    ("vp", (64,), b16), ("nth", (1,), f32), ("thf", (4,), f32),
     ("xi", (2816,), i32), ("xf", (2824,), f32), ("xl", (2824,), f32), ("w", (2816,), f32), ("wf", (176,), f32),
     ("wu", (176,), u16), ("w16", (176,), f16), ("cur", (176,), f32), ("dl", (528,), f32), ("q1", (352,), f32),
     ("q2", (176,), f32), ("eq", (528,), f32), ("pr", (528,), f32), ("cfin", (176,), f32),
-    ("cf", (512,), f32), ("wg0", (1024,), f32), ("wg1", (1024,), f32), ("mk0", (1024,), b16), ("mk1", (1024,), b16),
+    ("cf", (512,), f32), ("wg0", (1024,), b16), ("wg1", (1024,), b16), ("mk0", (1024,), b16), ("mk1", (1024,), b16),
     ("sm", (256,), f32), ("oo", (512,), u16), ("zb0", (1024,), f32), ("zb1", (1024,), f32), ("hb0", (1024,), f32),
     ("hb1", (1024,), f32), ("lb0", (1024,), f32), ("lb1", (1024,), f32), ("zz", (8, 4, 2, 128), f32), ("hs", (512,), f32),
     ("fe", (512,), f32), ("far", (512,), b16), ("inc", (512,), b16), ("cum", (512,), f32), ("pc", (512,), b16),
     ("et", (512,), f32), ("ea", (4096,), f32), ("ag", (2816,), f32), ("sg", (2816,), b16), ("tq", (176,), f32))}
 SCRATCH.update({n: ("dram", list(sh), d) for n, sh, d in (
-    ("l0d", (8, 128, 87), u16), ("l0r", (8, 128, 87), u16), ("l1d", (8, 128, 256), u16), ("l1r", (8, 128, 256), u16),
-    ("lrd", (8, 128, 66), u16), ("lrr", (8, 128, 66), u16), ("pxd", (16, 128, 176), i32), ("pxr", (16, 128, 176), i32),
-    ("rb", (4, 128, 176), i32), ("ro", (4, 128, 192), f32), ("od0", (8, 128, 192), f32), ("or0", (8, 128, 192), f32),
-    ("od1", (8, 128, 160), f32), ("or1", (8, 128, 160), f32), ("cd", (8, 128, 22), f32), ("cr", (8, 128, 22), f32))})
+    ("l0d", (8, 128, 64), u16), ("l0r", (8, 128, 64), u16), ("l1d", (8, 128, 256), u16), ("l1r", (8, 128, 256), u16),
+    ("lrd", (8, 128, 89), u16), ("lrr", (8, 128, 89), u16), ("pxd", (16, 128, 176), i32), ("pxr", (16, 128, 176), i32),
+    ("rb", (4, 128, 176), i32), ("ro0", (4, 128, 96), f32), ("od0", (16, 128, 96), f32), ("or0", (16, 128, 96), f32),
+    ("ro1", (4, 128, 80), f32), ("od1", (16, 128, 80), f32), ("or1", (16, 128, 80), f32),
+    ("cd", (8, 128, 22), f32), ("cr", (8, 128, 22), f32))})
 SCRATCH.update({n: ("psum", [128, k], f32) for n, k in (("pb", 3072), ("pw", 512), ("pv", 512))})
 PSUM = ["pb%d" % k for k in range(6)] + ["pw", "pv"]
-SEMAPHORES = (["v", "s", "t", "gc", "lsem", "l0a", "l1a", "lra", "ca", "rbi", "roi", "rlo"]
+SEMAPHORES = (["v", "s", "t", "gc", "lsem", "l0a", "l1a", "lra", "ca", "rbi", "ro0i", "ro1i", "rlo"]
               + [n + str(q) for n in ("pxa", "oa", "ob") for q in range(8)] + [n + str(c) for n in ("rg", "rk") for c in range(NC)]
               + ["ea0", "ea1", "dst", "dst1", "dl0", "dl1", "dpx", "dpy", "dlb", "dlc", "dxi", "dod0", "dod1", "dcd", "dy", "dz",
-                 "dsx", "dlr", "dlq"])
+                 "dlr", "dlq"])
 
 
 def layout(T, topo):
@@ -61,11 +63,11 @@ def transfer(topo, dst, mask, src, out, sem):
 def relay_program(g, core, T, topo, r, far):
     masks = two(topo.engines(core, T.cores[far[0]]), len(far))
     n = 2 * len(far)
-    for s, src, dst, to in (("rbi", T.rb, T.pxr[2 * r + 1], "pxa"), ("roi", T.ro, T.or0[r], "oa")):
+    for s, src, dst, to in (("rbi", T.rb, T.pxr, "pxa"), ("ro0i", T.ro0, T.or0, "oa"), ("ro1i", T.ro1, T.or1, "ob")):
         g.wait_ge(T.sem[s], n)
-        g.remote_dma_fused([transfer(topo, T.cores[q], masks[k], src[k], dst, T.sem[to + str(r)]) for k, q in enumerate(far)],
-                           local_sem=T.sem.rlo)
-    g.wait_ge(T.sem.rlo, 2 * n)
+        g.remote_dma_fused([transfer(topo, T.cores[q], masks[k], src[k], dst[2 * r + 1], T.sem[to + str(r)])
+                            for k, q in enumerate(far)], local_sem=T.sem.rlo)
+    g.wait_ge(T.sem.rlo, 3 * n)
 
 
 def rank_program(g, core, T, topo):
@@ -109,17 +111,15 @@ def rank_program(g, core, T, topo):
             wr[k] = [tag]
             rd[k] = {}
 
-    calls = {"act": g.scalar.activation, "iota": g.iota, "copy": g.vector.tensor_copy, "tt": g.vector.tensor_tensor,
-             "ts": g.vector.tensor_scalar, "set": g.vector.memset, "scan": g.vector.tensor_tensor_scan}
+    calls = {"mm": g.tensor.matmul, "acts": g.scalar.activation, "act": g.scalar.activation, "iota": g.iota,
+             "copy": g.vector.tensor_copy, "tt": g.vector.tensor_tensor, "ts": g.vector.tensor_scalar, "set": g.vector.memset,
+             "scan": g.vector.tensor_tensor_scan}
 
     def op(q, name, args, reads, writes, **kw):
         waits(q, deps_of(q, reads, writes))
         s = own[q]
-        if name == "mm":
-            for a in args:
-                ins = g.tensor.matmul(*a)
-        else:
-            ins = calls[name](*args, **kw)
+        for a in args if name in ("mm", "acts") else [args]:
+            ins = calls[name](*a, **kw)
         cnt[s] = cnt.get(s, 0) + 1
         ins.then_inc(sem[s], 1)
         done((s, cnt[s]), reads, writes)
@@ -159,6 +159,11 @@ def rank_program(g, core, T, topo):
     def to_all(src, dst, s):
         return to_far(lambda q: src[q], dst[rank], s) + to_near(lambda q: src[q], dst[rank], s, rest)
 
+    def halves(src, dst, s, via, vsem, kf, kn):
+        s = s + str(rank)
+        send(to_relay(lambda q: src[2 * q + 1], via, vsem) + to_far(lambda q: src[2 * q], dst[2 * rank], s), kf)
+        send(to_near(lambda q: src[2 * q], dst[2 * rank], s, rest) + to_near(lambda q: src[2 * q + 1], dst[2 * rank + 1], s, off), kn)
+
     lo, hi = 16 * rank, 16 * rank + 16
     npc = range(len(PIECES))
     others = [(a, b) for a, b in ((0, rank), (rank + 1, 8)) if b > a]
@@ -166,69 +171,55 @@ def rank_program(g, core, T, topo):
     def land(q, dst, src, mine, s, reads, key):
         dma(q, [(dst[16 * a:16 * b, :], src[a:b]) for a, b in others] + [(dst[lo:hi, :], mine[lo:hi, :])], s, reads, [key])
 
-    dma("y", [(T.sta[:], T.cand[:, 0:512]), (T.str0[:], T.ray[:, 0:176]), (T.sth[:], T.th[:])], "dst", [], ["sta", "str0", "sth"])
+    dma("y", [(T.sta[:], T.cand[:, 0:512]), (T["str"][:], T.ray[:]), (T.sth[:], T.th[:])], "dst", [], ["sta", "str", "sth"])
     fa, fb = far[0], far[-1] + 1
     na, nb = min(near + [rank]), max(near + [rank]) + 1
     dma("y", [(T.pxd[2 * fa:2 * fb], T.px[16 * fa:16 * fb, :])], "dpx", [], ["pxdf"])
+    dma("y", [(T.pxd[2 * na:2 * nb], T.px[16 * na:16 * nb, :])], "dpy", [], ["pxdn"])
+    dma("y", [(T.stb[:], T.cand[:, 512:1536]), (T.xi[lo:hi, :], T.px[lo:hi, :])], "dst1", [], ["stb", "xi.own"])
     op("g", "iota", (T.ia[:], [[-16, 8], [0, 16]], 0, 1), [], ["ia"])
     op("g", "iota", (T.ib[:], [[-16000, 8], [-999, 16]], 0, 1000), [], ["ib"])
     op("g", "iota", (T.vt[:, 0:1024], [[512, 8], [1, 128]], -2048, 0), [], ["vt0"], allow_small_or_imprecise_dtypes=True)
-
-    def selectors(ks):
-        for k in ks:
-            vts(T.uk[:, k, :], T.ia[:], float(k), None, (A.is_equal,), ["ia"], ["uk" if k == 15 else "uk.%d" % k])
-
-    op("v", "set", (T.ls0[:, 688:696], 0), [], ["ls0"])
-    selectors(range(8))
+    op("g", "iota", (T.ie[:], [[-1, 128]], 0, 1), [], ["ie"])
+    op("g", "iota", (T.io2[:], [[0, 8], [16, 8]], -64, 0), [], ["io2"])
+    op("g", "iota", (T.io3[:], [[0, 64]], 0, 1), [], ["io3"])
+    op("g", "iota", (T["id"][:], [[-1, 16], [-16, 8]], 0, 1), [], ["id"])
+    op("g", "iota", (T.ic[:], [[0, 16], [1, 8]], 1024, -1), [], ["ic"])
+    op("g", "iota", (T.ig[:], [[0, 8], [-8, 16]], 0, 1), [], ["ig"])
+    halves(T.pxd, T.pxr, "pxa", T.rb, "rbi", ["pxdf"], ["pxdn"])
+    for k in range(16):
+        vts(T.uk[:, k, :], T.ia[:], float(k), None, (A.is_equal,), ["ia"], ["uk" if k == 15 else "uk.%d" % k])
+    w16k, wfk, curk = ["w16.%d" % p for p in npc], ["wf%d" % p for p in npc], ["cur%d" % p for p in npc]
+    vts(T.w16[:], T["str"][:, 0:176], -2048.0, None, (A.add,), ["str"], w16k)
     for m in range(2):
         for c in range(NC):
             k = c * 128 + m * 64
             op("v", "copy", (T.ls0[:, k:k + 64], T.sta[:, m, :, c, :]), ["sta"], ["ls0.%d" % k])
-    op("v", "copy", (T.ls0[:, 512:688], T.str0[:]), ["str0"], ["ls0.r"])
-    vts(T.sth2[:, 0:1], T.sth[:], 10, None, (A.arith_shift_right,), ["sth"], ["sth2a"])
-    vts(T.sth2[:, 1:2], T.sth[:], 1023, None, (A.bitwise_and,), ["sth"], ["sth2b"])
-    op("v", "copy", (T.ls0[:, 688:690], T.sth2[:]), ["sth2a", "sth2b"], ["ls0"])
-    ls0k = ["ls0", "ls0.r"] + ["ls0.%d" % k for k in range(0, 512, 64)]
-    dma("y", [(T.l0d[:], T.ls0[:])], "dlb", ls0k, ["l0d"])
-    dma("y", [(T.pxd[2 * na:2 * nb], T.px[16 * na:16 * nb, :])], "dpy", [], ["pxdn"])
-    dma("y", [(T.str1[:], T.ray[:, 176:704]), (T.stb[:], T.cand[:, 512:1536])], "dst1", [], ["stb", "str1"])
-    send(to_all(T.l0d, T.l0r, "l0a"), ["l0d"])
-    ps = "pxa%d" % rank
-    send(to_relay(lambda q: T.pxd[2 * q + 1], T.rb, "rbi") + to_far(lambda q: T.pxd[2 * q], T.pxr[2 * rank], ps), ["pxdf"])
-    send(to_near(lambda q: T.pxd[2 * q], T.pxr[2 * rank], ps, rest)
-         + to_near(lambda q: T.pxd[2 * q + 1], T.pxr[2 * rank + 1], ps, off), ["pxdn"])
-    selectors(range(8, 16))
+    ls0k = ["ls0.%d" % k for k in range(0, 512, 64)]
     for k in range(16):
-        vts(T.dkf[:, k, :], T.ib[:], float(k), -U, (A.is_equal, A.mult), ["ib"], ["dkf" if k == 15 else "dkf.%d" % k])
-    op("v", "copy", (T.dkb[:], T.dkf[:]), ["dkf"], ["dkb"])
-    for c in range(1, NC):
-        vts(T.vt[:, 1024 * c:1024 * c + 1024], T.vt[:, 0:1024], 128.0 * c, None, (A.add,), ["vt0"], ["vt%d" % c])
-    op("g", "iota", (T.io2[:], [[128, 4], [512, 8], [16, 8]], -2048, 0), [], ["io2"])
-    op("g", "iota", (T.io3[:], [[0, 256]], 0, 1), [], ["io3"])
-    op("g", "iota", (T.ia[:], [[-1, 16], [-16, 8]], 0, 1), [], ["ia"])
-    op("g", "iota", (T.ib[:], [[-1, 128]], 0, 1), [], ["ib"])
-    op("g", "iota", (T.ic[:], [[0, 16], [1, 8]], 1024, -1), [], ["ic"])
+        vts(T.dkb[:, k, :], T.ib[:], float(k), -U, (A.is_equal, A.mult), ["ib"], ["dkb" if k == 15 else "dkb.%d" % k])
     vts(T.io3[:], T.io3[:], 15, None, (A.bitwise_and,), ["io3"], ["io3"])
-    vts(T.ic[:], T.ic[:], 7, None, (A.bitwise_and,), ["ic"], ["ic"])
+    vts(T.ni[:], T.ie[:], 0.0, -0.25, (A.is_equal, A.mult), ["ie"], ["ni"])
     op("v", "tt", (T.io2[:], T.io2[:], T.io3[:], A.add), ["io2", "io3"], ["io2"])
-    vts(T.pmx[:], T.ia[:], 0.0, None, (A.is_equal,), ["ia"], ["pmx"])
-    vts(T.idf[:], T.ib[:], 0.0, None, (A.is_equal,), ["ib"], ["idf"])
-    vts(T.ni[:], T.ib[:], 0.0, -0.25, (A.is_equal, A.mult), ["ib"], ["ni"])
-    vts(T.ob[:], T.ic[:], 0.0, None, (A.is_equal,), ["ic"], ["ob"])
-    vts(T.vp[:], T.io2[:], U, None, (A.mult,), ["io2"], ["vp"])
-    op("v", "set", (T.ones[:], 1.0), [], ["ones"])
     op("v", "set", (T.six[:], 64.0), [], ["six"])
-    op("v", "set", (T.xl[:, 2816:2824], float(BIG)), [], ["xls"])
-    op("v", "set", (T.xf[:, 2816:2824], float(-BIG)), [], ["xfs"])
-    op("v", "set", (T.cur[:], 0.0), [], ["cur%d" % p for p in npc])
-    op("v", "copy", (T.lsr[:], T.str1[:]), ["str1"], ["lsr"])
-    dma("s", [(T.lrd[:], T.lsr[:])], "dlr", ["lsr"], ["lrd"])
-    arrives("l0a", 14, "l0r")
-    land("y", T.ll0, T.l0r, T.ls0, "dl0", ["l0r"] + ls0k, "ll0")
-    send(to_all(T.lrd, T.lrr, "lra"), ["lrd"])
-    w16k, wfk, curk = ["w16.%d" % p for p in npc], ["wf%d" % p for p in npc], ["cur%d" % p for p in npc]
-    vts(T.w16[:], T.ll0[:, 512:688], -2048.0, None, (A.add,), ["ll0"], w16k)
-    op("v", "copy", (T.wf[:], T.ll0[:, 512:688]), ["ll0"], wfk)
+    vts(T.vp[:], T.io2[:], -4 * U, None, (A.mult,), ["io2"], ["vp"])
+
+    def constants():
+        op("v", "set", (T.lsr[:, 704:712], 0), [], ["lsr"])
+        vts(T.sth2[:, 0:1], T.sth[:], 10, None, (A.arith_shift_right,), ["sth"], ["sth2a"])
+        vts(T.sth2[:, 1:2], T.sth[:], 1023, None, (A.bitwise_and,), ["sth"], ["sth2b"])
+        op("v", "copy", (T.lsr[:, 0:704], T["str"][:]), ["str"], ["lsr.r"])
+        op("v", "copy", (T.lsr[:, 704:706], T.sth2[:]), ["sth2a", "sth2b"], ["lsr"])
+        dma("s", [(T.lrd[:], T.lsr[:])], "dlr", ["lsr", "lsr.r"], ["lrd"])
+        vts(T.ic[:], T.ic[:], 7, None, (A.bitwise_and,), ["ic"], ["ic"])
+        vts(T.pmx[:], T["id"][:], 0.0, None, (A.is_equal,), ["id"], ["pmx"])
+        op("v", "set", (T.ones[:], 1.0), [], ["ones"])
+        vts(T.ob[:], T.ic[:], 0.0, None, (A.is_equal,), ["ic"], ["ob"])
+        op("v", "set", (T.xl[:, 2816:2824], float(BIG)), [], ["xls"])
+        op("v", "set", (T.xf[:, 2816:2824], float(-BIG)), [], ["xfs"])
+        op("v", "set", (T.cur[:], 0.0), [], curk)
+        for b in range(KB):
+            vts(T.es[:, b, :], T.ig[:], float(b), None, (A.is_equal,), ["ig"], ["es" if b == KB - 1 else "es.%d" % b])
 
     def later_lists():
         vts(T.stc[:], T.stb[:], 4, None, (A.arith_shift_right,), ["stb"], ["stc"])
@@ -248,25 +239,21 @@ def rank_program(g, core, T, topo):
         land("y", T.ll1, T.l1r, T.ls1, "dl1", ["l1r"] + ls1k, "ll1")
 
     def thresholds():
-        op("v", "copy", (T.thf[:, 0:2], T.ll0[:, 688:690]), ["ll0"], ["thf"])
+        op("v", "copy", (T.thf[:, 0:2], T.llr[:, 704:706]), ["llr"], ["thf"])
         vts(T.thf[:, 2:3], T.thf[:, 0:1], 1024.0, None, (A.mult,), ["thf"], ["thf2"])
         op("v", "tt", (T.thf[:, 3:4], T.thf[:, 2:3], T.thf[:, 1:2], A.add), ["thf", "thf2"], ["thf3"])
         op("t", "mm", [(T.pb[:, 2048:2049], T.pmx[:], T.thf[:, 3:4], True, True)], ["pmx", "thf3"], ["pb4"])
         vts(T.nth[:], T.pb[:, 2048:2049], -1.0, None, (A.mult,), ["pb4"], ["nth"])
 
-    dma("y", [(T.xi[lo:hi, :], T.px[lo:hi, :])], "dsx", [], ["xi.own"])
     for q in near + far:
         arrives("pxa%d" % q, 4, "pxr%d" % q)
         dma("y", [(T.xi[16 * q:16 * q + 16, :], T.pxr[2 * q:2 * q + 2])], "dxi", ["pxr%d" % q], ["xi.%d" % q])
     xik = ["xi.own", "xi.%d" % far[-1]]
     wk = ["w%d" % b for b in range(8)]
 
-    def unpack(t):
-        if t == 0:
-            parts = [(512 * b, min(512 * b + 512, R)) for b in range(6)]
-        else:
-            parts = [(352 * b, 352 * b + 352) for b in range(8)]
-        for n, (a, b) in enumerate(parts):
+    def unpack(t, ns):
+        for n in ns:
+            a, b = (512 * n, min(512 * n + 512, R)) if t == 0 else (352 * n, 352 * n + 352)
             ps, key = ((T.pw, "pw"), (T.pv, "pv"))[n % 2]
             if t == 0:
                 mm = [(ps[:, k:b - a:16], T.uk[:, k, :], T.w16[:, a // 16:b // 16], True, True) for k in range(16)]
@@ -276,28 +263,29 @@ def rank_program(g, core, T, topo):
             op("s", "act", (T.w[:, a:b], ps[:, 0:b - a], F.Copy), [key], [wk[n]])
 
     def lists(t, where=0):
-        return (T.ll0, 0, "ll0") if t == 0 else (T.ll1, 512 * (t - 1) + 1024 * where, "ll1")
+        return (T.ls0, 0, ls0k) if t == 0 else (T.ll1, 512 * (t - 1) + 1024 * where, ["ll1"])
 
     def prepare(t):
         buf, base, key = lists(t)
-        op("v", "copy", (T.cf[:], buf[:, base:base + 512]), [key], ["cf"])
+        op("v", "copy", (T.cf[:], buf[:, base:base + 512]), key, ["cf"])
 
-    turn = [0]
+    turn = {"s": 0, "v": 0}
 
     def look(t, c, m, q):
         buf, base, key = lists(t, 1)
         k = base + c * 128 + m * 64
         out, ok = T.pb[:, 512 * c + 64 * m:512 * c + 64 * m + 64], "pb%d" % c
-        win = T.w[:, 0:R].indirect(buf[:, k:k + 64])
+        turn[q] ^= 1
         if q == "s":
-            wg, wgk = (T.wg0, T.wg1)[c % 2], "wg%d" % (c % 2)
-            op("s", "act", (wg[:], win, F.Copy), [key] + wk, [wgk])
-            op("t", "mm", [(out, T.idf[:], T.vp[:, c * 64:c * 64 + 64], True, False)]
-               + [(out, T.dkf[:, i, :], wg[:, i:1024:16], False, i == 15) for i in range(16)], ["dkf", "idf", "vp", wgk], [ok])
+            wg, wgk = (T.wg0, T.wg1)[turn[q]], "wg%d" % turn[q]
+            op("s", "acts", [(wg[:, 128 * b:128 * b + 128], T.w[:, 0:R].indirect(buf[:, k + 8 * b:k + 8 * b + 8]), F.Copy,
+                              float(2048 - 64 - 512 * b - 128 * c)) for b in range(8)], key + wk, [wgk])
+            op("t", "mm", [(out, T.ni[:], T.vp[:], True, False)]
+               + [(out, T.dkb[:, i, :], wg[:, i:1024:16], False, i == 15) for i in range(16)], ["dkb", "ni", "vp", wgk], [ok])
         else:
-            turn[0] ^= 1
-            mk, mkk = (T.mk0, T.mk1)[turn[0]], "mk%d" % turn[0]
-            op("v", "tt", (mk[:], win, T.vt[:, c * 1024:c * 1024 + 1024], A.is_ge), [key, "vt%d" % c] + wk, [mkk])
+            mk, mkk = (T.mk0, T.mk1)[turn[q]], "mk%d" % turn[q]
+            op("v", "tt", (mk[:], T.w[:, 0:R].indirect(buf[:, k:k + 64]), T.vt[:, c * 1024:c * 1024 + 1024], A.is_ge),
+               key + ["vt%d" % c] + wk, [mkk])
             op("t", "mm", [(out, T.six[0:1, :], T.six[0:1, 0:64], True, False)]
                + [(out, T.dkb[:, i, :], mk[:, i:1024:16], False, i == 15) for i in range(16)], ["dkb", "six", mkk], [ok])
 
@@ -309,18 +297,23 @@ def rank_program(g, core, T, topo):
     xfk = ["xf%d" % p for p in npc] + ["xfs"]
     xlk = ["xl%d" % p for p in npc] + ["xls"]
 
-    def see0(c):
-        e, d = c % 2, slice(c * 128, c * 128 + 64)
-        for z, f, n in ((T.ag[:, 1024 * e:1024 * e + 1024], F.Copy, ["za%d" % e] + ["ag%d" % p for p in npc]),
-                        ((T.zb0, T.zb1)[e][:], F.Abs, ["zb%d" % e])):
-            op("s", "act", (z, T.xf[:, 0:2824].indirect(T.oo[:, d]), f), ["oo%d" % c] + xfk, n)
+    def masked(t, c):
+        return (T.om, "om") if t == 0 else (T.oo, "oo%d" % c)
 
-    def see1(c):
+    def see0(c, t=1):
+        e, d = c % 2, slice(c * 128, c * 128 + 64)
+        o, ok = masked(t, c)
+        za = T.ag[:, 1024 * e:1024 * e + 1024]
+        op("s", "act", (za, T.xf[:, 0:2824].indirect(o[:, d]), F.Copy), [ok] + xfk, ["za%d" % e, "ag0", "agh", "ag1"])
+        op("s", "act", ((T.zb0, T.zb1)[e][:], za, F.Abs), ["za%d" % e], ["zb%d" % e])
+
+    def see1(c, t=1):
         e, d = c % 2, slice(c * 128 + 64, c * 128 + 128)
+        o, ok = masked(t, c)
         za, zb, hb, lb = T.ag[:, 1024 * e:1024 * e + 1024], (T.zb0, T.zb1)[e], (T.hb0, T.hb1)[e], (T.lb0, T.lb1)[e]
-        op("v", "tt", (hb[:], T.xf[:, 0:2824].indirect(T.oo[:, d]), za, A.max), ["oo%d" % c, "za%d" % e] + xfk, ["hb%d" % e])
+        op("v", "tt", (hb[:], T.xf[:, 0:2824].indirect(o[:, d]), za, A.max), [ok, "za%d" % e] + xfk, ["hb%d" % e])
         dma("y", [(T.zz[:, a, c, 0, :], hb[16 * a:16 * a + 16, :]) for a in range(8)], "rg%d" % c, ["hb%d" % e], ["zh%d" % c])
-        op("v", "tt", (lb[:], T.xl[:, 0:2824].indirect(T.oo[:, d]), zb[:], A.min), ["oo%d" % c, "zb%d" % e] + xlk, ["lb%d" % e])
+        op("v", "tt", (lb[:], T.xl[:, 0:2824].indirect(o[:, d]), zb[:], A.min), [ok, "zb%d" % e] + xlk, ["lb%d" % e])
         dma("y", [(T.zz[:, a, c, 1, :], lb[16 * a:16 * a + 16, :]) for a in range(8)], "rk%d" % c, ["lb%d" % e], ["zl%d" % c])
 
     def reduce(c0, c1):
@@ -328,11 +321,10 @@ def rank_program(g, core, T, topo):
             for j, o, z in ((0, A.max, "zh"), (1, A.min, "zl")):
                 b = 2048 + 512 * j
                 acc, key = T.pb[:, b + 128 * c0:b + 128 * c1], "pb%d" % (4 + j)
-                x, src = T.zz[:, a, c0:c1, j, :], [z + str(c) for c in range(c0, c1)]
+                src = [z + str(c) for c in range(c0, c1)]
                 if a == 1:
-                    op("v", "tt", (acc, T.zz[:, 0, c0:c1, j, :], x, o), src, [key])
-                else:
-                    op("v", "tt", (acc, acc, x, o), src + [key], [key])
+                    op("s", "act", (acc, T.zz[:, 0, c0:c1, j, :], F.Copy), src, [key])
+                op("v", "tt", (acc, acc, T.zz[:, a, c0:c1, j, :], o), src + [key], [key])
 
     def carve():
         op("s", "act", (T.hs[:], T.pb[:, 2048:2560], F.Identity, T.nth[:]), ["pb4", "nth"], ["hs"])
@@ -344,14 +336,20 @@ def rank_program(g, core, T, topo):
         op("v", "tt", (T.pv[:], T.inc[:], T.fe[:], A.mult), ["inc", "fe"], ["pv"])
         vts(T.pc[:], T.cum[:], 128.0, None, (A.is_le,), ["cum"], ["pc"])
         op("v", "tt", (T.et[:], T.pc[:], T.pv[:], A.mult), ["pc", "pv"], ["et"])
-        dma("y", [(T.ea[16 * a:16 * a + 16, :], T.et[:]) for a in range(0, 4)], "ea0", ["et"], ["eaa"])
-        dma("s", [(T.ea[16 * a:16 * a + 16, :], T.et[:]) for a in range(4, 8)], "ea1", ["et"], ["eab"])
+        pairs = [(T.ea[16 * a:16 * a + 16, 512 * b:512 * b + 512], T.et[b:128:8, :]) for b in range(KB, 8) for a in range(8)]
+        n = len(pairs) * 5 // 8
+        dma("y", pairs[:n], "ea0", ["et"], ["eaa"])
+        dma("s", pairs[n:], "ea1", ["et"], ["eab"])
+        for b in range(KB):
+            d = slice(512 * b, 512 * b + 512)
+            op("t", "mm", [(T.pb[:, d], T.es[:, b, :], T.et[:], True, True)], ["es", "et"], ["pb%d" % b])
+            op("s", "act", (T.ea[:, d], T.pb[:, d], F.Copy), ["pb%d" % b], ["eac"])
 
     dl = T.dl
 
     def places(t):
         if t == 0:
-            op("v", "copy", (T.eq[:], T.llr[:]), ["llr"], ["eq0", "eq1", "eq2"])
+            op("v", "copy", (T.eq[:], T.llr[:, 176:704]), ["llr"], ["eq0", "eq1", "eq2"])
             op("v", "tt", (T.pr[:, 0:176], T.eq[:, 0:176], T.wf[:], A.subtract), ["eq0"] + wfk, ["pr.0"])
             op("v", "tt", (T.pr[:, 176:528], T.eq[:, 176:528], T.eq[:, 0:352], A.subtract), ["eq0"], ["pr"])
             vts(dl[:], T.pr[:], 1.0 / U, None, (A.mult,), ["pr.0", "pr"], ["dl"])
@@ -364,7 +362,7 @@ def rank_program(g, core, T, topo):
         op("v", "tt", (T.pr[:, 0:352], T.eq[:, 0:352], dl[:, 176:528], A.mult), ["eq0", "eq1", "dl"], ["pr"])
         op("v", "tt", (T.q2[:], T.pr[:, 0:176], T.pr[:, 176:352], A.add), ["pr"], ["q2"])
 
-    pgs = [((T.pw, "pw"), (T.pv, "pv"))[p % 2] for p in npc]
+    pgs = ((T.pw, "pw"), (T.pv, "pv"))
 
     def span(p):
         return 16 * PIECES[p][0], 16 * PIECES[p][1]
@@ -373,12 +371,20 @@ def rank_program(g, core, T, topo):
         a, b = span(p)
         return [(k, 512 * k, min(512 * k + 512, R)) for k in range(a // 512, (b + 511) // 512)]
 
+    def agk(p):
+        return ["ag0", "agh"] if p == 0 else ["ag1"]
+
     def gather(p, q):
         a, b = span(p)
-        out, src = T.ag[:, a:b], T.ea[:, 0:V].indirect(T.wu[:, a // 16:b // 16])
-        args, name = ((out, src, F.Copy), "act") if q == "s" else ((out, src), "copy")
-        op(q, name, args, ["eaa", "eab", "wu%d" % p], ["ag%d" % p, "za0", "za1"])
-        op("s", "act", (T.sg[:, a:b], out, F.Sign), ["ag%d" % p], ["sg%d" % p])
+        h = (a + b) // 2
+        parts = (("v", a, h, ["agh"]), ("s", h, b, ["ag0"])) if q == "vs" else ((q, a, b, agk(p)),)
+        for q, x, y, keys in parts:
+            args = (T.ag[:, x:y], T.ea[:, 0:V].indirect(T.wu[:, x // 16:y // 16]))
+            op(q, "act" if q == "s" else "copy", args + ((F.Copy,) if q == "s" else ()), ["eaa", "eab", "eac", "wu%d" % p], keys)
+
+    def sign(p):
+        a, b = span(p)
+        op("s", "act", (T.sg[:, a:b], T.ag[:, a:b], F.Sign), agk(p), ["sg%d" % p])
 
     def pack(p):
         a, b = PIECES[p]
@@ -386,8 +392,8 @@ def rank_program(g, core, T, topo):
         op("t", "mm", [(ps[:, a:b], T.dkb[:, k, :], T.sg[:, 16 * a + k:16 * b:16], k == 0, k == 15) for k in range(16)],
            ["dkb", "sg%d" % p], [key])
 
-    def spread(p):
-        for k, x, y in banks(p):
+    def spread(p, ks=slice(0, 6)):
+        for k, x, y in banks(p)[ks]:
             op("t", "mm", [(T.pb[:, x:y], T.ones[0:1, 0:128], T.ones[0:1, 0:y - x], True, False),
                            (T.pb[:, x:y], T.ni[:], T.sg[:, x:y], False, True)], ["ni", "ones", "sg%d" % p], ["pb%d" % k])
 
@@ -411,9 +417,10 @@ def rank_program(g, core, T, topo):
         a, b = span(p)
         pk = ["pb%d" % k for k, _, _ in banks(p)]
         if part == 0:
-            op("v", "tt", (T.pb[:, a:b], T.xf[:, a:b], T.pb[:, a:b], A.mult), pk + ["xf%d" % p], pk)
+            for k, x, y in banks(p):
+                op("v", "tt", (T.pb[:, x:y], T.xf[:, x:y], T.pb[:, x:y], A.mult), ["pb%d" % k, "xf%d" % p], ["pb%d" % k])
         elif part == 1:
-            op("v", "tt", (T.xi[:, a:b], T.pb[:, a:b], T.ag[:, a:b], A.add), pk + ["ag%d" % p], ["xi%d" % p])
+            op("v", "tt", (T.xi[:, a:b], T.pb[:, a:b], T.ag[:, a:b], A.add), pk + agk(p), ["xi%d" % p])
         else:
             vts(T.xf[:, a:b], T.xi[:, a:b], 0.0, float(TOP), (A.max, A.min), ["xi%d" % p], ["xf%d" % p])
 
@@ -421,39 +428,48 @@ def rank_program(g, core, T, topo):
         a, b = span(p)
         op("s", "act", (T.xl[:, a:b], T.xf[:, a:b], F.Copy), ["xf%d" % p], ["xl%d" % p])
 
-    op("v", "copy", (T.wu[:], T.wf[:]), wfk, ["wu%d" % p for p in npc])
-    unpack(0)
+    unpack(0, range(6))
     for t in range(3):
         if t == 0:
             prepare(0)
             for c in range(NC):
-                look(0, c, 0, "v")
+                if c:
+                    vts(T.vt[:, 1024 * c:1024 * c + 1024], T.vt[:, 0:1024], 128.0 * c, None, (A.add,), ["vt0"], ["vt%d" % c])
+                look(0, c, 0, "s")
                 look(0, c, 1, "v")
                 if c:
                     mask(c - 1)
             mask(NC - 1)
-            thresholds()
+            ook = ["oo%d" % c for c in range(NC)]
+            dma("s", [(T.l0d[:], T.oo[:])], "dlb", ook, ["l0d"])
+            send(to_all(T.l0d, T.l0r, "l0a"), ["l0d"])
+            constants()
+            send(to_all(T.lrd, T.lrr, "lra"), ["lrd"])
             for p in npc:
                 a, b = span(p)
                 op("v", "copy", (T.xf[:, a:b], T.xi[:, a:b]), xik, ["xf%d" % p])
                 second(p)
-            for c in range(NC):
-                see0(c)
-                see1(c)
+            arrives("l0a", 14, "l0r")
+            land("y", T.om, T.l0r, T.oo, "dl0", ["l0r"] + ook, "om")
             arrives("lra", 14, "lrr")
-            land("y", T.llr, T.lrr, T.lsr, "dlq", ["lrr", "lsr"], "llr")
+            land("y", T.llr, T.lrr, T.lsr, "dlq", ["lrr", "lsr", "lsr.r"], "llr")
+            for c in range(NC):
+                see0(c, 0)
+                see1(c, 0)
+            thresholds()
+            op("v", "copy", (T.wf[:], T.llr[:, 0:176]), ["llr"], wfk)
+            op("v", "copy", (T.wu[:], T.llr[:, 0:176]), ["llr"], ["wu%d" % p for p in npc])
+            reduce(0, 3)
+            reduce(3, 4)
         else:
-            for c in range(NC + 2):
-                if c < NC:
-                    look(t, c, 0, LOOK[c])
-                    look(t, c, 1, "v")
-                if 1 <= c <= NC:
-                    mask(c - 1)
-                    see0(c - 1)
-                if c >= 2:
-                    see1(c - 2)
-        reduce(0, NC - 1)
-        reduce(NC - 1, NC)
+            for s in SCHED.split():
+                c = int(s[1])
+                if s[0] == "L":
+                    look(t, c, int(s[2]), s[3])
+                elif s[0] == "R":
+                    reduce(c, int(s[2]))
+                else:
+                    {"M": mask, "Z": see0, "V": see1, "X": second}[s[0]](c)
         carve()
         places(t)
         if t == 0:
@@ -463,43 +479,41 @@ def rank_program(g, core, T, topo):
         for step in range(2):
             end = step == 1
             last = end and t == 2
-            gather(0, "s")
-            for p in npc[1:]:
-                gather(p, "s" if step or p > 1 else "v")
-            for p in npc:
-                pack(p)
-                spread(p)
+            gather(0, "s" if step else "vs")
+            sign(0)
+            gather(1, "s" if step else "v")
+            sign(1)
+            pack(0)
+            spread(0)
+            pack(1)
             small(0, t, step, last)
-            for p in npc:
-                move(p, 0)
-                if p + 1 < len(PIECES):
-                    small(p + 1, t, step, last)
-                elif last:
-                    vts(T.cfin[:], T.cur[:], 1.0 / U, 3.0, (A.mult, A.min), curk, ["cfin"])
-                move(p, 1)
-                move(p, 2)
+            move(0, 0)
+            small(1, t, step, last)
             if end and t < 2:
-                for p in npc[:-1]:
-                    second(p)
-                unpack(t + 1)
-                if t == 0:
-                    prepare(1)
-                second(npc[-1])
-    w0 = 16 * CUT
-    first = ["xf%d" % p for p in npc if PIECES[p][1] <= CUT]
-    later = ["xf%d" % p for p in npc if PIECES[p][1] > CUT]
-    dma("y", [(T.od0[:], T.xf[:, 0:w0])], "dod0", first, ["od0"])
+                for k in range(3):
+                    spread(1, slice(k, k + 1))
+                    unpack(t + 1, ((0, 1, 2, 3), (4, 5, 6, 7), ())[k])
+            else:
+                spread(1)
+            if last:
+                vts(T.cfin[:], T.cur[:], 1.0 / U, 3.0, (A.mult, A.min), curk, ["cfin"])
+            for p, part in ((0, 1), (0, 2), (1, 0), (1, 1), (1, 2)):
+                move(p, part)
+            if end and t == 0:
+                prepare(1)
+    w0 = span(0)[1]
     dma("s", [(T.cd[:], T.cfin[:])], "dcd", ["cfin"], ["cd"])
-    dma("y", [(T.od1[:], T.xf[:, w0:R])], "dod1", later, ["od1"])
-    send(to_relay(lambda q: T.od0[q], T.ro, "roi") + to_near(lambda q: T.od0[q], T.or0[rank], "oa%d" % rank, off), ["od0"])
+    dma("y", [(T.od0[:], T.xf[:, 0:w0])], "dod0", ["xf0"], ["od0"])
+    dma("y", [(T.od1[:], T.xf[:, w0:R])], "dod1", ["xf1"], ["od1"])
+    halves(T.od0, T.or0, "oa", T.ro0, "ro0i", ["od0"], ["od0"])
+    halves(T.od1, T.or1, "ob", T.ro1, "ro1i", ["od1"], ["od1"])
     send(to_all(T.cd, T.cr, "ca"), ["cd"])
-    send(to_all(T.od1, T.or1, "ob%d" % rank), ["od1"])
     dma("s", [(T.yx[lo:hi, 0:w0], T.xf[lo:hi, 0:w0]), (T.yx[lo:hi, w0:R], T.xf[lo:hi, w0:R]),
-              (T.yc[lo:hi, :], T.cfin[lo:hi, :])], "dz", first + later + ["cfin"], [])
-    arrives("ca", 14, "cr")
-    dma("s", [(T.yc[16 * a:16 * b, :], T.cr[a:b]) for a, b in others], "dz", ["cr"], [])
+              (T.yc[lo:hi, :], T.cfin[lo:hi, :])], "dz", ["xf0", "xf1", "cfin"], [])
     for s, src, dst, q0, d in (("oa", T.or0, slice(0, w0), "y", "dy"), ("ob", T.or1, slice(w0, R), "s", "dz")):
         for q in near + far:
-            arrives(s + str(q), 2, s + ".%d" % q)
-            dma(q0, [(T.yx[16 * q:16 * q + 16, dst], src[q])], d, [s + ".%d" % q], [])
+            arrives(s + str(q), 4, s + ".%d" % q)
+            dma(q0, [(T.yx[16 * q:16 * q + 16, dst], src[2 * q:2 * q + 2])], d, [s + ".%d" % q], [])
+    arrives("ca", 14, "cr")
+    dma("s", [(T.yc[16 * a:16 * b, :], T.cr[a:b]) for a, b in others], "dz", ["cr"], [])
     waits("g", [(s, cnt[s]) for s in cnt])

from concourse.bass import DstId, RemoteDMATransfer
from concourse.mybir import dt, AluOpType, AxisListType, ActivationFunctionType

A = AluOpType
F = ActivationFunctionType
R, V, TOP, BIG = 2816, 4096, 2 ** 20 - 1, 2 ** 22
U = 4096.0
NC = 4
PIECES = ((0, 96), (96, 176))
KB = 3
SCHED = "L00s L01v X0 L10s X1 L11v M0 Z0 M1 L20s V0 L21v Z1 L30s L31v M2 V1 Z2 M3 V2 Z3 V3 R03 R34"
f32, i32, u16, f16, b16 = "float32", "int32", "uint16", "float16", "bfloat16"
SCRATCH = {n: ("sbuf", [128] + list(sh), d) for n, sh, d in (
    ("sta", (2, 8, 4, 8), i32), ("stb", (4, 8, 4, 8), i32), ("stc", (4, 8, 4, 8), i32), ("str", (704,), i32),
    ("sth", (1,), i32), ("sth2", (2,), i32), ("ls0", (512,), u16), ("ls1", (2048,), u16),
    ("lsr", (712,), u16), ("ll1", (2048,), u16), ("llr", (712,), u16), ("om", (512,), u16),
    ("ia", (128,), i32), ("ib", (128,), i32), ("ic", (128,), i32), ("id", (128,), i32), ("ie", (128,), i32),
    ("ig", (128,), i32), ("es", (3, 128), f32), ("io2", (64,), i32), ("io3", (64,), i32),
    ("uk", (16, 128), f16), ("dkb", (16, 128), b16), ("ob", (128,), b16), ("ni", (128,), b16),
    ("pmx", (128,), f32), ("ones", (512,), b16), ("six", (128,), b16), ("vt", (4096,), f32),
    ("vp", (64,), b16), ("nth", (1,), f32), ("thf", (4,), f32),
    ("xi", (2816,), i32), ("xf", (2824,), f32), ("xl", (2824,), f32), ("w", (2816,), f32), ("wf", (176,), f32),
    ("wu", (176,), u16), ("w16", (176,), f16), ("cur", (176,), f32), ("dl", (528,), f32), ("q1", (352,), f32),
    ("q2", (176,), f32), ("eq", (528,), f32), ("pr", (528,), f32), ("cfin", (176,), f32),
    ("cf", (512,), f32), ("wg0", (1024,), b16), ("wg1", (1024,), b16), ("mk0", (1024,), b16), ("mk1", (1024,), b16),
    ("sm", (256,), f32), ("oo", (512,), u16), ("zb0", (1024,), f32), ("zb1", (1024,), f32), ("hb0", (1024,), f32),
    ("hb1", (1024,), f32), ("lb0", (1024,), f32), ("lb1", (1024,), f32), ("zz", (8, 4, 2, 128), f32), ("hs", (512,), f32),
    ("fe", (512,), f32), ("far", (512,), b16), ("inc", (512,), b16), ("cum", (512,), f32), ("pc", (512,), b16),
    ("et", (512,), f32), ("ea", (4096,), f32), ("ag", (2816,), f32), ("sg", (2816,), b16), ("tq", (176,), f32))}
SCRATCH.update({n: ("dram", list(sh), d) for n, sh, d in (
    ("l0d", (8, 128, 64), u16), ("l0r", (8, 128, 64), u16), ("l1d", (8, 128, 256), u16), ("l1r", (8, 128, 256), u16),
    ("lrd", (8, 128, 89), u16), ("lrr", (8, 128, 89), u16), ("pxd", (16, 128, 176), i32), ("pxr", (16, 128, 176), i32),
    ("rb", (4, 128, 176), i32), ("ro0", (4, 128, 96), f32), ("od0", (16, 128, 96), f32), ("or0", (16, 128, 96), f32),
    ("ro1", (4, 128, 80), f32), ("od1", (16, 128, 80), f32), ("or1", (16, 128, 80), f32),
    ("cd", (8, 128, 22), f32), ("cr", (8, 128, 22), f32))})
SCRATCH.update({n: ("psum", [128, k], f32) for n, k in (("pb", 3072), ("pw", 512), ("pv", 512))})
PSUM = ["pb%d" % k for k in range(6)] + ["pw", "pv"]
SEMAPHORES = (["v", "s", "t", "gc", "lsem", "l0a", "l1a", "lra", "ca", "rbi", "ro0i", "ro1i", "rlo"]
              + [n + str(q) for n in ("pxa", "oa", "ob") for q in range(8)] + [n + str(c) for n in ("rg", "rk") for c in range(NC)]
              + ["ea0", "ea1", "dst", "dst1", "dl0", "dl1", "dpx", "dpy", "dlb", "dlc", "dxi", "dod0", "dod1", "dcd", "dy", "dz",
                 "dlr", "dlq"])


def layout(T, topo):
    lay = []
    for r, c in enumerate(T.cores):
        mine = [q for q, d in enumerate(T.cores) if topo.chip(d) == topo.chip(c)]
        far = [q for q in range(len(T.cores)) if q not in mine]
        other = [d for d in topo.cores_of(c) if topo.die(d) != topo.die(c)]
        lay.append(([q for q in mine if q != r], far, other[mine.index(r)]))
    return lay


def two(engines, n):
    return [(1 << engines[2 * k]) | (1 << engines[2 * k + 1]) for k in range(n)]


def transfer(topo, dst, mask, src, out, sem):
    rid, pid, _ = topo.addr(dst)
    return RemoteDMATransfer(dst_ids=[DstId(rid=rid, pnc=pid)], dma_engine_mask=mask, remote_sem=sem, src=src, dst=out)


def relay_program(g, core, T, topo, r, far):
    masks = two(topo.engines(core, T.cores[far[0]]), len(far))
    n = 2 * len(far)
    for s, src, dst, to in (("rbi", T.rb, T.pxr, "pxa"), ("ro0i", T.ro0, T.or0, "oa"), ("ro1i", T.ro1, T.or1, "ob")):
        g.wait_ge(T.sem[s], n)
        g.remote_dma_fused([transfer(topo, T.cores[q], masks[k], src[k], dst[2 * r + 1], T.sem[to + str(r)])
                            for k, q in enumerate(far)], local_sem=T.sem.rlo)
    g.wait_ge(T.sem.rlo, 3 * n)


def rank_program(g, core, T, topo):
    lay = layout(T, topo)
    rank = T.rank_of(core)
    if rank is None:
        for r, (near, far, rel) in enumerate(lay):
            if rel == core:
                relay_program(g, core, T, topo, r, far)
        return
    near, far, rel = lay[rank]
    sem = T.sem
    queue = {"v": g.vector, "s": g.scalar, "t": g.tensor, "y": g.sync, "g": g}
    own = {"v": "v", "s": "s", "t": "t", "g": "gc"}
    cnt, seen, wr, rd = {}, {}, {}, {}

    def waits(q, deps):
        need = {}
        for s, n in deps:
            need[s] = max(need.get(s, 0), n)
        for s in need:
            if seen.get((q, s), 0) < need[s]:
                queue[q].wait_ge(sem[s], need[s])
                seen[(q, s)] = need[s]

    def deps_of(q, reads, writes):
        d = []
        for k in reads + writes:
            d += wr.get(k, [])
        for k in writes:
            d += rd.get(k, {}).items()
        for k in reads:
            if k in PSUM:
                d += [(s, n) for s, n in rd.get(k, {}).items() if s != own.get(q)]
        return d

    def done(tag, reads, writes):
        for k in reads:
            rd.setdefault(k, {})[tag[0]] = tag[1]
        for k in writes:
            wr[k] = [tag]
            rd[k] = {}

    calls = {"mm": g.tensor.matmul, "acts": g.scalar.activation, "act": g.scalar.activation, "iota": g.iota,
             "copy": g.vector.tensor_copy, "tt": g.vector.tensor_tensor, "ts": g.vector.tensor_scalar, "set": g.vector.memset,
             "scan": g.vector.tensor_tensor_scan}

    def op(q, name, args, reads, writes, **kw):
        waits(q, deps_of(q, reads, writes))
        s = own[q]
        for a in args if name in ("mm", "acts") else [args]:
            ins = calls[name](*a, **kw)
        cnt[s] = cnt.get(s, 0) + 1
        ins.then_inc(sem[s], 1)
        done((s, cnt[s]), reads, writes)

    def vts(out, in0, s1, s2, ops, reads, writes):
        op("v", "ts", (out, in0, s1, s2) + ops, reads, writes)

    def dma(q, pairs, s, reads, writes):
        waits(q, deps_of(q, reads, writes))
        for o, i in pairs:
            queue[q].dma_start(o, i).then_inc(sem[s], 16)
        cnt[s] = cnt.get(s, 0) + 16 * len(pairs)
        done((s, cnt[s]), reads, writes)

    def arrives(s, n, key):
        cnt[s] = cnt.get(s, 0) + n
        wr[key] = [(s, cnt[s])]

    nf, nn = len(far), len(near)
    off = topo.engines(core, T.cores[far[0]])
    rest = [e for e in topo.engines(core, T.cores[near[0]]) if e not in off]

    def send(moves, reads):
        waits("g", deps_of("g", reads, []))
        g.remote_dma_fused([transfer(topo, d, m, a, b, sem[s]) for d, m, a, b, s in moves], local_sem=sem.lsem)
        cnt["lsem"] = cnt.get("lsem", 0) + 2 * len(moves)

    def to_far(src, dst, s):
        return [(T.cores[q], m, src(q), dst, s) for q, m in zip(far, two(off, nf))]

    def to_relay(src, via, vsem):
        return [(rel, m, src(q), via[k], vsem) for k, (q, m) in enumerate(zip(far, two(rest, nf)))]

    def to_near(src, dst, s, engines):
        return [(T.cores[q], m, src(q), dst, s) for q, m in zip(near, two(engines, nn))]

    def to_all(src, dst, s):
        return to_far(lambda q: src[q], dst[rank], s) + to_near(lambda q: src[q], dst[rank], s, rest)

    def halves(src, dst, s, via, vsem, kf, kn):
        s = s + str(rank)
        send(to_relay(lambda q: src[2 * q + 1], via, vsem) + to_far(lambda q: src[2 * q], dst[2 * rank], s), kf)
        send(to_near(lambda q: src[2 * q], dst[2 * rank], s, rest) + to_near(lambda q: src[2 * q + 1], dst[2 * rank + 1], s, off), kn)

    lo, hi = 16 * rank, 16 * rank + 16
    npc = range(len(PIECES))
    others = [(a, b) for a, b in ((0, rank), (rank + 1, 8)) if b > a]

    def land(q, dst, src, mine, s, reads, key):
        dma(q, [(dst[16 * a:16 * b, :], src[a:b]) for a, b in others] + [(dst[lo:hi, :], mine[lo:hi, :])], s, reads, [key])

    dma("y", [(T.sta[:], T.cand[:, 0:512]), (T["str"][:], T.ray[:]), (T.sth[:], T.th[:])], "dst", [], ["sta", "str", "sth"])
    fa, fb = far[0], far[-1] + 1
    na, nb = min(near + [rank]), max(near + [rank]) + 1
    dma("y", [(T.pxd[2 * fa:2 * fb], T.px[16 * fa:16 * fb, :])], "dpx", [], ["pxdf"])
    dma("y", [(T.pxd[2 * na:2 * nb], T.px[16 * na:16 * nb, :])], "dpy", [], ["pxdn"])
    dma("y", [(T.stb[:], T.cand[:, 512:1536]), (T.xi[lo:hi, :], T.px[lo:hi, :])], "dst1", [], ["stb", "xi.own"])
    op("g", "iota", (T.ia[:], [[-16, 8], [0, 16]], 0, 1), [], ["ia"])
    op("g", "iota", (T.ib[:], [[-16000, 8], [-999, 16]], 0, 1000), [], ["ib"])
    op("g", "iota", (T.vt[:, 0:1024], [[512, 8], [1, 128]], -2048, 0), [], ["vt0"], allow_small_or_imprecise_dtypes=True)
    op("g", "iota", (T.ie[:], [[-1, 128]], 0, 1), [], ["ie"])
    op("g", "iota", (T.io2[:], [[0, 8], [16, 8]], -64, 0), [], ["io2"])
    op("g", "iota", (T.io3[:], [[0, 64]], 0, 1), [], ["io3"])
    op("g", "iota", (T["id"][:], [[-1, 16], [-16, 8]], 0, 1), [], ["id"])
    op("g", "iota", (T.ic[:], [[0, 16], [1, 8]], 1024, -1), [], ["ic"])
    op("g", "iota", (T.ig[:], [[0, 8], [-8, 16]], 0, 1), [], ["ig"])
    halves(T.pxd, T.pxr, "pxa", T.rb, "rbi", ["pxdf"], ["pxdn"])
    for k in range(16):
        vts(T.uk[:, k, :], T.ia[:], float(k), None, (A.is_equal,), ["ia"], ["uk" if k == 15 else "uk.%d" % k])
    w16k, wfk, curk = ["w16.%d" % p for p in npc], ["wf%d" % p for p in npc], ["cur%d" % p for p in npc]
    vts(T.w16[:], T["str"][:, 0:176], -2048.0, None, (A.add,), ["str"], w16k)
    for m in range(2):
        for c in range(NC):
            k = c * 128 + m * 64
            op("v", "copy", (T.ls0[:, k:k + 64], T.sta[:, m, :, c, :]), ["sta"], ["ls0.%d" % k])
    ls0k = ["ls0.%d" % k for k in range(0, 512, 64)]
    for k in range(16):
        vts(T.dkb[:, k, :], T.ib[:], float(k), -U, (A.is_equal, A.mult), ["ib"], ["dkb" if k == 15 else "dkb.%d" % k])
    vts(T.io3[:], T.io3[:], 15, None, (A.bitwise_and,), ["io3"], ["io3"])
    vts(T.ni[:], T.ie[:], 0.0, -0.25, (A.is_equal, A.mult), ["ie"], ["ni"])
    op("v", "tt", (T.io2[:], T.io2[:], T.io3[:], A.add), ["io2", "io3"], ["io2"])
    op("v", "set", (T.six[:], 64.0), [], ["six"])
    vts(T.vp[:], T.io2[:], -4 * U, None, (A.mult,), ["io2"], ["vp"])

    def constants():
        op("v", "set", (T.lsr[:, 704:712], 0), [], ["lsr"])
        vts(T.sth2[:, 0:1], T.sth[:], 10, None, (A.arith_shift_right,), ["sth"], ["sth2a"])
        vts(T.sth2[:, 1:2], T.sth[:], 1023, None, (A.bitwise_and,), ["sth"], ["sth2b"])
        op("v", "copy", (T.lsr[:, 0:704], T["str"][:]), ["str"], ["lsr.r"])
        op("v", "copy", (T.lsr[:, 704:706], T.sth2[:]), ["sth2a", "sth2b"], ["lsr"])
        dma("s", [(T.lrd[:], T.lsr[:])], "dlr", ["lsr", "lsr.r"], ["lrd"])
        vts(T.ic[:], T.ic[:], 7, None, (A.bitwise_and,), ["ic"], ["ic"])
        vts(T.pmx[:], T["id"][:], 0.0, None, (A.is_equal,), ["id"], ["pmx"])
        op("v", "set", (T.ones[:], 1.0), [], ["ones"])
        vts(T.ob[:], T.ic[:], 0.0, None, (A.is_equal,), ["ic"], ["ob"])
        op("v", "set", (T.xl[:, 2816:2824], float(BIG)), [], ["xls"])
        op("v", "set", (T.xf[:, 2816:2824], float(-BIG)), [], ["xfs"])
        op("v", "set", (T.cur[:], 0.0), [], curk)
        for b in range(KB):
            vts(T.es[:, b, :], T.ig[:], float(b), None, (A.is_equal,), ["ig"], ["es" if b == KB - 1 else "es.%d" % b])

    def later_lists():
        vts(T.stc[:], T.stb[:], 4, None, (A.arith_shift_right,), ["stb"], ["stc"])
        for half in range(2):
            for m in range(4):
                for c in range(NC):
                    k = half * 1024 + (m // 2) * 512 + c * 128 + (m % 2) * 64
                    op("v", "copy", (T.ls1[:, k:k + 64], T.stb[:, m, :, c, :]), ["stb"], ["ls1.%d" % k])
            if half == 0:
                vts(T.stb[:], T.stb[:], 15, None, (A.bitwise_and,), ["stb"], ["stb"])
                vts(T.stb[:], T.stb[:], 176.0, None, (A.mult,), ["stb"], ["stb"])
                op("v", "tt", (T.stb[:], T.stb[:], T.stc[:], A.add), ["stb", "stc"], ["stb"])
        ls1k = ["ls1.%d" % k for k in range(0, 2048, 64)]
        dma("y", [(T.l1d[:], T.ls1[:])], "dlc", ls1k, ["l1d"])
        send(to_all(T.l1d, T.l1r, "l1a"), ["l1d"])
        arrives("l1a", 14, "l1r")
        land("y", T.ll1, T.l1r, T.ls1, "dl1", ["l1r"] + ls1k, "ll1")

    def thresholds():
        op("v", "copy", (T.thf[:, 0:2], T.llr[:, 704:706]), ["llr"], ["thf"])
        vts(T.thf[:, 2:3], T.thf[:, 0:1], 1024.0, None, (A.mult,), ["thf"], ["thf2"])
        op("v", "tt", (T.thf[:, 3:4], T.thf[:, 2:3], T.thf[:, 1:2], A.add), ["thf", "thf2"], ["thf3"])
        op("t", "mm", [(T.pb[:, 2048:2049], T.pmx[:], T.thf[:, 3:4], True, True)], ["pmx", "thf3"], ["pb4"])
        vts(T.nth[:], T.pb[:, 2048:2049], -1.0, None, (A.mult,), ["pb4"], ["nth"])

    for q in near + far:
        arrives("pxa%d" % q, 4, "pxr%d" % q)
        dma("y", [(T.xi[16 * q:16 * q + 16, :], T.pxr[2 * q:2 * q + 2])], "dxi", ["pxr%d" % q], ["xi.%d" % q])
    xik = ["xi.own", "xi.%d" % far[-1]]
    wk = ["w%d" % b for b in range(8)]

    def unpack(t, ns):
        for n in ns:
            a, b = (512 * n, min(512 * n + 512, R)) if t == 0 else (352 * n, 352 * n + 352)
            ps, key = ((T.pw, "pw"), (T.pv, "pv"))[n % 2]
            if t == 0:
                mm = [(ps[:, k:b - a:16], T.uk[:, k, :], T.w16[:, a // 16:b // 16], True, True) for k in range(16)]
            else:
                mm = [(ps[:, 176 * k:176 * k + 176], T.uk[:, 2 * n + k, :], T.w16[:], True, True) for k in range(2)]
            op("t", "mm", mm, ["uk"] + w16k, [key])
            op("s", "act", (T.w[:, a:b], ps[:, 0:b - a], F.Copy), [key], [wk[n]])

    def lists(t, where=0):
        return (T.ls0, 0, ls0k) if t == 0 else (T.ll1, 512 * (t - 1) + 1024 * where, ["ll1"])

    def prepare(t):
        buf, base, key = lists(t)
        op("v", "copy", (T.cf[:], buf[:, base:base + 512]), key, ["cf"])

    turn = {"s": 0, "v": 0}

    def look(t, c, m, q):
        buf, base, key = lists(t, 1)
        k = base + c * 128 + m * 64
        out, ok = T.pb[:, 512 * c + 64 * m:512 * c + 64 * m + 64], "pb%d" % c
        turn[q] ^= 1
        if q == "s":
            wg, wgk = (T.wg0, T.wg1)[turn[q]], "wg%d" % turn[q]
            op("s", "acts", [(wg[:, 128 * b:128 * b + 128], T.w[:, 0:R].indirect(buf[:, k + 8 * b:k + 8 * b + 8]), F.Copy,
                              float(2048 - 64 - 512 * b - 128 * c)) for b in range(8)], key + wk, [wgk])
            op("t", "mm", [(out, T.ni[:], T.vp[:], True, False)]
               + [(out, T.dkb[:, i, :], wg[:, i:1024:16], False, i == 15) for i in range(16)], ["dkb", "ni", "vp", wgk], [ok])
        else:
            mk, mkk = (T.mk0, T.mk1)[turn[q]], "mk%d" % turn[q]
            op("v", "tt", (mk[:], T.w[:, 0:R].indirect(buf[:, k:k + 64]), T.vt[:, c * 1024:c * 1024 + 1024], A.is_ge),
               key + ["vt%d" % c] + wk, [mkk])
            op("t", "mm", [(out, T.six[0:1, :], T.six[0:1, 0:64], True, False)]
               + [(out, T.dkb[:, i, :], mk[:, i:1024:16], False, i == 15) for i in range(16)], ["dkb", "six", mkk], [ok])

    def mask(c):
        d, e, k = slice(c * 128, c * 128 + 128), slice(c % 2 * 128, c % 2 * 128 + 128), "sm%d" % (c % 2)
        op("v", "tt", (T.sm[:, e], T.pb[:, 512 * c:512 * c + 128], T.cf[:, d], A.max), ["pb%d" % c, "cf"], [k])
        vts(T.oo[:, d], T.sm[:, e], float(R), None, (A.min,), [k], ["oo%d" % c])

    xfk = ["xf%d" % p for p in npc] + ["xfs"]
    xlk = ["xl%d" % p for p in npc] + ["xls"]

    def masked(t, c):
        return (T.om, "om") if t == 0 else (T.oo, "oo%d" % c)

    def see0(c, t=1):
        e, d = c % 2, slice(c * 128, c * 128 + 64)
        o, ok = masked(t, c)
        za = T.ag[:, 1024 * e:1024 * e + 1024]
        op("s", "act", (za, T.xf[:, 0:2824].indirect(o[:, d]), F.Copy), [ok] + xfk, ["za%d" % e, "ag0", "agh", "ag1"])
        op("s", "act", ((T.zb0, T.zb1)[e][:], za, F.Abs), ["za%d" % e], ["zb%d" % e])

    def see1(c, t=1):
        e, d = c % 2, slice(c * 128 + 64, c * 128 + 128)
        o, ok = masked(t, c)
        za, zb, hb, lb = T.ag[:, 1024 * e:1024 * e + 1024], (T.zb0, T.zb1)[e], (T.hb0, T.hb1)[e], (T.lb0, T.lb1)[e]
        op("v", "tt", (hb[:], T.xf[:, 0:2824].indirect(o[:, d]), za, A.max), [ok, "za%d" % e] + xfk, ["hb%d" % e])
        dma("y", [(T.zz[:, a, c, 0, :], hb[16 * a:16 * a + 16, :]) for a in range(8)], "rg%d" % c, ["hb%d" % e], ["zh%d" % c])
        op("v", "tt", (lb[:], T.xl[:, 0:2824].indirect(o[:, d]), zb[:], A.min), [ok, "zb%d" % e] + xlk, ["lb%d" % e])
        dma("y", [(T.zz[:, a, c, 1, :], lb[16 * a:16 * a + 16, :]) for a in range(8)], "rk%d" % c, ["lb%d" % e], ["zl%d" % c])

    def reduce(c0, c1):
        for a in range(1, 8):
            for j, o, z in ((0, A.max, "zh"), (1, A.min, "zl")):
                b = 2048 + 512 * j
                acc, key = T.pb[:, b + 128 * c0:b + 128 * c1], "pb%d" % (4 + j)
                src = [z + str(c) for c in range(c0, c1)]
                if a == 1:
                    op("s", "act", (acc, T.zz[:, 0, c0:c1, j, :], F.Copy), src, [key])
                op("v", "tt", (acc, acc, T.zz[:, a, c0:c1, j, :], o), src + [key], [key])

    def carve():
        op("s", "act", (T.hs[:], T.pb[:, 2048:2560], F.Identity, T.nth[:]), ["pb4", "nth"], ["hs"])
        op("v", "tt", (T.far[:], T.hs[:], T.pb[:, 2560:3072], A.is_gt), ["hs", "pb5"], ["far"])
        op("s", "act", (T.fe[:], T.pb[:, 2560:3072], F.Copy, -0.375, -0.25), ["pb5"], ["fe"])
        op("t", "mm", [(T.pw[:], T.ob[:], T.far[:], True, True)], ["ob", "far"], ["pw"])
        vts(T.inc[:], T.pw[:], 9.0, None, (A.is_ge,), ["pw"], ["inc"])
        op("v", "scan", (T.cum[:], T.inc[:], T.inc[:], 0.0, A.add, A.max), ["inc"], ["cum"])
        op("v", "tt", (T.pv[:], T.inc[:], T.fe[:], A.mult), ["inc", "fe"], ["pv"])
        vts(T.pc[:], T.cum[:], 128.0, None, (A.is_le,), ["cum"], ["pc"])
        op("v", "tt", (T.et[:], T.pc[:], T.pv[:], A.mult), ["pc", "pv"], ["et"])
        pairs = [(T.ea[16 * a:16 * a + 16, 512 * b:512 * b + 512], T.et[b:128:8, :]) for b in range(KB, 8) for a in range(8)]
        n = len(pairs) * 5 // 8
        dma("y", pairs[:n], "ea0", ["et"], ["eaa"])
        dma("s", pairs[n:], "ea1", ["et"], ["eab"])
        for b in range(KB):
            d = slice(512 * b, 512 * b + 512)
            op("t", "mm", [(T.pb[:, d], T.es[:, b, :], T.et[:], True, True)], ["es", "et"], ["pb%d" % b])
            op("s", "act", (T.ea[:, d], T.pb[:, d], F.Copy), ["pb%d" % b], ["eac"])

    dl = T.dl

    def places(t):
        if t == 0:
            op("v", "copy", (T.eq[:], T.llr[:, 176:704]), ["llr"], ["eq0", "eq1", "eq2"])
            op("v", "tt", (T.pr[:, 0:176], T.eq[:, 0:176], T.wf[:], A.subtract), ["eq0"] + wfk, ["pr.0"])
            op("v", "tt", (T.pr[:, 176:528], T.eq[:, 176:528], T.eq[:, 0:352], A.subtract), ["eq0"], ["pr"])
            vts(dl[:], T.pr[:], 1.0 / U, None, (A.mult,), ["pr.0", "pr"], ["dl"])
            return
        for k in range(3):
            vts(T.eq[:, k * 176:k * 176 + 176], T.cur[:], U * k, None, (A.is_equal,), curk, ["eq%d" % k])
        op("v", "tt", (T.pr[:], T.eq[:], dl[:], A.mult), ["eq0", "eq1", "eq2", "dl"], ["pr"])
        op("v", "tt", (T.q1[:, 176:352], T.pr[:, 0:176], T.pr[:, 176:352], A.add), ["pr"], ["q1t"])
        op("v", "tt", (T.q1[:, 0:176], T.q1[:, 176:352], T.pr[:, 352:528], A.add), ["pr", "q1t"], ["q1"])
        op("v", "tt", (T.pr[:, 0:352], T.eq[:, 0:352], dl[:, 176:528], A.mult), ["eq0", "eq1", "dl"], ["pr"])
        op("v", "tt", (T.q2[:], T.pr[:, 0:176], T.pr[:, 176:352], A.add), ["pr"], ["q2"])

    pgs = ((T.pw, "pw"), (T.pv, "pv"))

    def span(p):
        return 16 * PIECES[p][0], 16 * PIECES[p][1]

    def banks(p):
        a, b = span(p)
        return [(k, 512 * k, min(512 * k + 512, R)) for k in range(a // 512, (b + 511) // 512)]

    def agk(p):
        return ["ag0", "agh"] if p == 0 else ["ag1"]

    def gather(p, q):
        a, b = span(p)
        h = (a + b) // 2
        parts = (("v", a, h, ["agh"]), ("s", h, b, ["ag0"])) if q == "vs" else ((q, a, b, agk(p)),)
        for q, x, y, keys in parts:
            args = (T.ag[:, x:y], T.ea[:, 0:V].indirect(T.wu[:, x // 16:y // 16]))
            op(q, "act" if q == "s" else "copy", args + ((F.Copy,) if q == "s" else ()), ["eaa", "eab", "eac", "wu%d" % p], keys)

    def sign(p):
        a, b = span(p)
        op("s", "act", (T.sg[:, a:b], T.ag[:, a:b], F.Sign), agk(p), ["sg%d" % p])

    def pack(p):
        a, b = PIECES[p]
        ps, key = pgs[p]
        op("t", "mm", [(ps[:, a:b], T.dkb[:, k, :], T.sg[:, 16 * a + k:16 * b:16], k == 0, k == 15) for k in range(16)],
           ["dkb", "sg%d" % p], [key])

    def spread(p, ks=slice(0, 6)):
        for k, x, y in banks(p)[ks]:
            op("t", "mm", [(T.pb[:, x:y], T.ones[0:1, 0:128], T.ones[0:1, 0:y - x], True, False),
                           (T.pb[:, x:y], T.ni[:], T.sg[:, x:y], False, True)], ["ni", "ones", "sg%d" % p], ["pb%d" % k])

    def small(p, t, step, last):
        a, b = PIECES[p]
        ps, key = pgs[p]
        if t == 0:
            q, qk = dl[:, 176 * step + a:176 * step + b], "dl"
        else:
            q, qk = (T.q1[:, a:b], "q1") if step == 0 else (T.q2[:, a:b], "q2")
        wfp, tqp = ["wf%d" % p], ["tq%d" % p]
        if not last:
            op("v", "tt", (T.tq[:, a:b], ps[:, a:b], q, A.mult), [key, qk], tqp)
            op("v", "tt", (T.wf[:, a:b], T.wf[:, a:b], T.tq[:, a:b], A.add), wfp + tqp, wfp)
            if step == 1:
                vts(T.w16[:, a:b], T.wf[:, a:b], -2048.0, None, (A.add,), wfp, ["w16.%d" % p])
            op("v", "copy", (T.wu[:, a:b], T.wf[:, a:b]), wfp, ["wu%d" % p])
        op("v", "tt", (T.cur[:, a:b], ps[:, a:b], T.cur[:, a:b], A.add), [key, "cur%d" % p], ["cur%d" % p])

    def move(p, part):
        a, b = span(p)
        pk = ["pb%d" % k for k, _, _ in banks(p)]
        if part == 0:
            for k, x, y in banks(p):
                op("v", "tt", (T.pb[:, x:y], T.xf[:, x:y], T.pb[:, x:y], A.mult), ["pb%d" % k, "xf%d" % p], ["pb%d" % k])
        elif part == 1:
            op("v", "tt", (T.xi[:, a:b], T.pb[:, a:b], T.ag[:, a:b], A.add), pk + agk(p), ["xi%d" % p])
        else:
            vts(T.xf[:, a:b], T.xi[:, a:b], 0.0, float(TOP), (A.max, A.min), ["xi%d" % p], ["xf%d" % p])

    def second(p):
        a, b = span(p)
        op("s", "act", (T.xl[:, a:b], T.xf[:, a:b], F.Copy), ["xf%d" % p], ["xl%d" % p])

    unpack(0, range(6))
    for t in range(3):
        if t == 0:
            prepare(0)
            for c in range(NC):
                if c:
                    vts(T.vt[:, 1024 * c:1024 * c + 1024], T.vt[:, 0:1024], 128.0 * c, None, (A.add,), ["vt0"], ["vt%d" % c])
                look(0, c, 0, "s")
                look(0, c, 1, "v")
                if c:
                    mask(c - 1)
            mask(NC - 1)
            ook = ["oo%d" % c for c in range(NC)]
            dma("s", [(T.l0d[:], T.oo[:])], "dlb", ook, ["l0d"])
            send(to_all(T.l0d, T.l0r, "l0a"), ["l0d"])
            constants()
            send(to_all(T.lrd, T.lrr, "lra"), ["lrd"])
            for p in npc:
                a, b = span(p)
                op("v", "copy", (T.xf[:, a:b], T.xi[:, a:b]), xik, ["xf%d" % p])
                second(p)
            arrives("l0a", 14, "l0r")
            land("y", T.om, T.l0r, T.oo, "dl0", ["l0r"] + ook, "om")
            arrives("lra", 14, "lrr")
            land("y", T.llr, T.lrr, T.lsr, "dlq", ["lrr", "lsr", "lsr.r"], "llr")
            for c in range(NC):
                see0(c, 0)
                see1(c, 0)
            thresholds()
            op("v", "copy", (T.wf[:], T.llr[:, 0:176]), ["llr"], wfk)
            op("v", "copy", (T.wu[:], T.llr[:, 0:176]), ["llr"], ["wu%d" % p for p in npc])
            reduce(0, 3)
            reduce(3, 4)
        else:
            for s in SCHED.split():
                c = int(s[1])
                if s[0] == "L":
                    look(t, c, int(s[2]), s[3])
                elif s[0] == "R":
                    reduce(c, int(s[2]))
                else:
                    {"M": mask, "Z": see0, "V": see1, "X": second}[s[0]](c)
        carve()
        places(t)
        if t == 0:
            later_lists()
        elif t == 1:
            prepare(2)
        for step in range(2):
            end = step == 1
            last = end and t == 2
            gather(0, "s" if step else "vs")
            sign(0)
            gather(1, "s" if step else "v")
            sign(1)
            pack(0)
            spread(0)
            pack(1)
            small(0, t, step, last)
            move(0, 0)
            small(1, t, step, last)
            if end and t < 2:
                for k in range(3):
                    spread(1, slice(k, k + 1))
                    unpack(t + 1, ((0, 1, 2, 3), (4, 5, 6, 7), ())[k])
            else:
                spread(1)
            if last:
                vts(T.cfin[:], T.cur[:], 1.0 / U, 3.0, (A.mult, A.min), curk, ["cfin"])
            for p, part in ((0, 1), (0, 2), (1, 0), (1, 1), (1, 2)):
                move(p, part)
            if end and t == 0:
                prepare(1)
    w0 = span(0)[1]
    dma("s", [(T.cd[:], T.cfin[:])], "dcd", ["cfin"], ["cd"])
    dma("y", [(T.od0[:], T.xf[:, 0:w0])], "dod0", ["xf0"], ["od0"])
    dma("y", [(T.od1[:], T.xf[:, w0:R])], "dod1", ["xf1"], ["od1"])
    halves(T.od0, T.or0, "oa", T.ro0, "ro0i", ["od0"], ["od0"])
    halves(T.od1, T.or1, "ob", T.ro1, "ro1i", ["od1"], ["od1"])
    send(to_all(T.cd, T.cr, "ca"), ["cd"])
    dma("s", [(T.yx[lo:hi, 0:w0], T.xf[lo:hi, 0:w0]), (T.yx[lo:hi, w0:R], T.xf[lo:hi, w0:R]),
              (T.yc[lo:hi, :], T.cfin[lo:hi, :])], "dz", ["xf0", "xf1", "cfin"], [])
    for s, src, dst, q0, d in (("oa", T.or0, slice(0, w0), "y", "dy"), ("ob", T.or1, slice(w0, R), "s", "dz")):
        for q in near + far:
            arrives(s + str(q), 4, s + ".%d" % q)
            dma(q0, [(T.yx[16 * q:16 * q + 16, dst], src[2 * q:2 * q + 2])], d, [s + ".%d" % q], [])
    arrives("ca", 14, "cr")
    dma("s", [(T.yc[16 * a:16 * b, :], T.cr[a:b]) for a, b in others], "dz", ["cr"], [])
    waits("g", [(s, cnt[s]) for s in cnt])
